import numpy as np, ml_dtypes
CORES = [24,25,26,27,28,29,30,31]
N = 8
BF = ml_dtypes.bfloat16
def gentries(a):
    return np.ascontiguousarray(a.reshape(8, 16, -1).transpose(0, 2, 1)).reshape(8, -1)
def gtable(e):
    e = np.asarray(e); return np.ascontiguousarray(e.reshape(8, -1, 16).transpose(0, 2, 1)).reshape(128, -1).astype(np.int32)
V, R = 2048, 4
def family(rng, sizes, depth, pool, mix, fall=None):
    key = np.tile(np.arange(V), (N, 1)); lev = np.zeros(V, np.int64); comp = np.zeros(V, np.int64); via = [-1] * V; o = rng.permutation(V); a = 0
    for i in range(len(sizes)):
        s, D = int(sizes[i]), int(depth[i]); m = o[a:a + s]; a += s; comp[m] = i
        if s == 1: continue
        root = int(np.min(m)); m = m[m != root]; l = np.concatenate([np.arange(1, D + 1), rng.integers(1, D + 1, s - 1 - D)])
        if fall is not None and fall[i]: m = np.sort(m)[::-1]; l = np.sort(l)
        lev[m] = l
        at = [[root]] + [[] for k in range(D)]
        for c, k in zip(m.tolist(), l.tolist()): at[k].append(c)
        for k in range(1, D + 1):
            for c in at[k]:
                p = at[k - 1][int(rng.integers(len(at[k - 1])))]; w = [q for q in pool if q != via[p]]; q = w[int(rng.integers(len(w)))]
                key[q, c] = key[q, p]; via[c] = q
    for q in range(N if mix > 0 else 0):
        h = np.flatnonzero(key[q] == np.arange(V)); t = comp[h] * (R + 1) + lev[h]; keep = rng.random(h.size) >= mix
        hk, tk = h[keep], t[keep]; s = np.argsort(tk, kind="stable"); hk, tk = hk[s], tk[s]
        lo = np.searchsorted(tk, t, "left"); n = np.searchsorted(tk, t, "right") - lo; z = ~keep & (n > 0)
        to = h + 0; to[z] = hk[lo[z] + (rng.random(np.count_nonzero(z)) * n[z]).astype(np.int64)]
        jump = np.arange(V); jump[h] = to; key[q] = jump[key[q]]
    return key
def lay(rng, key, way):
    if way == 0: o = np.lexsort((rng.random(V), rng.permutation(V)[key]))
    elif way == 1: o = np.lexsort((np.arange(V), key))
    else: o = np.lexsort((-np.arange(V), -key))
    k = key[o]; s = np.ones(V, np.int64); s[1:] = k[1:] != k[:-1]
    e = np.append(np.flatnonzero(s)[1:], V) - 1; last = np.zeros(V, np.int64); last[o] = e[np.add.accumulate(s) - 1]
    return [o, s, last]
def pack(rng, keys, ways):
    a = np.array([[lay(rng, keys[g][q], ways[q, g]) for g in range(8)] for q in range(N)])
    return {"pm": np.stack([gtable(u) for u in a[:, :, 0]]), "en": np.stack([gtable(u) for u in a[:, :, 2]]), "st": np.ascontiguousarray(a[:, :, 1]).astype(np.int32)}
def depths(rng, s):
    top = np.minimum(R, s - 1); D = np.where(top > 0, 1 + (rng.random(s.size) * top).astype(np.int64), 0); i = np.argmax(s); D[i] = top[i]; return D
def some(rng):
    out = []
    for n in rng.choice(np.arange(6, 41), 8, replace=False):
        c = np.sort(rng.choice(V - 1, int(n) - 1, replace=False)) + 1; s = np.diff(np.concatenate([[0], c, [V]]))
        out.append(family(rng, s, depths(rng, s), list(range(N)), rng.choice([0.0, 0.05, 0.15])))
    return out
def setup_inputs(rng):
    return pack(rng, some(rng), np.zeros((N, 8), np.int64))
def setup_inputs_deep(rng):
    few = rng.permutation(8)[:4]; n = rng.choice(np.arange(V // (2 * (R + 1)), V // (R + 1) + 1), 8, replace=False); keys = []
    for g in range(8):
        m = int(n[g]); s = [R + 1] * m + [1] * (V - m * (R + 1)); pool = rng.permutation(N)[:2].tolist() if g in few else list(range(N))
        keys.append(family(rng, s, [R] * m + [0] * (V - m * (R + 1)), pool, 0.0, np.arange(len(s)) % 2 == 0))
    return pack(rng, keys, np.zeros((N, 8), np.int64))
def setup_inputs_ends(rng):
    keys = some(rng); w = rng.permutation(8); one = np.tile(np.arange(V), (N, 1))
    keys[w[0]][rng.integers(N)] = 0
    keys[w[1]] = one + 0
    keys[w[2]] = np.tile(rng.integers(0, 30, V), (N, 1))
    keys[w[3]] = one + 0; keys[w[3]][rng.integers(N)] = rng.integers(0, 3, V)
    x = np.concatenate([[0], 1 + rng.choice(V - 2, R - 1, replace=False), [V - 1]]); k = one + 0; ab = rng.permutation(N)[:2]
    for i in range(R): k[ab[i % 2], x[i + 1]] = x[i]
    keys[w[4]] = k
    return pack(rng, keys, np.zeros((N, 8), np.int64))
def setup_inputs_order(rng):
    return pack(rng, some(rng), rng.integers(1, 3, (N, 8)))
def setup_inputs_spread(rng):
    keys = []; half = int(rng.integers(8))
    for g in range(8):
        s = [1] * (V // 2 if g == half else 0); left = V - len(s)
        while left > 0:
            t = max(1, int(left * (0.3 + 0.4 * rng.random()))); s.append(t); left -= t
        s = np.array(s); keys.append(family(rng, s, depths(rng, s), list(range(N)) + [int(rng.integers(N))] * (3 * N), rng.choice([0.0, 0.3, 0.8])))
    return pack(rng, keys, np.zeros((N, 8), np.int64))
def hop(p, st, L):
    g = np.arange(8)[:, None]; M = L
    for q in range(N):
        s = st[q].reshape(-1); m = np.minimum.reduceat(L[g, p[q]].reshape(-1), np.flatnonzero(s))
        u = np.empty_like(L); u[g, p[q]] = m[np.add.accumulate(s) - 1].reshape(8, V); M = np.minimum(M, u)
    return M
def check_inputs(d):
    p = np.stack([gentries(a) for a in d["pm"]]); e = np.stack([gentries(a) for a in d["en"]]); s = d["st"]
    if not (np.sort(p, -1) == np.arange(V)).all(): return ["pm: every vertex once"]
    if not (((s == 0) | (s == 1)).all() and (s[:, :, 0] == 1).all()): return ["st: 0 and 1, beginning with 1"]
    bad = []; t = s.reshape(-1); last = ((np.append(np.flatnonzero(t)[1:], t.size) - 1) % V)[np.add.accumulate(t) - 1].reshape(N, 8, V)
    if not (np.take_along_axis(e, p, 2) == last).all(): bad.append("en: last places")
    L = np.tile(np.arange(V), (8, 1))
    for i in range(R): L = hop(p, s, L)
    if not (hop(p, s, L) == L).all(): bad.append("at most R steps to the smallest vertex")
    return bad
def reference(pm, en, st):
    p = np.stack([gentries(a) for a in pm]); L = np.tile(np.arange(V), (8, 1))
    while True:
        M = hop(p, st, L)
        if (M == L).all(): break
        L = M
    c = np.count_nonzero(L == np.arange(V), axis=1).reshape(8, 1)
    return {"y": np.stack([L for r in range(N)]).astype(np.float32), "cnt": np.stack([c for r in range(N)]).astype(np.float32)}

@@ -1,0 +1,268 @@
+import math
+from concourse.bass import DstId, RemoteDMATransfer
+from concourse.mybir import AluOpType as A, AxisListType, ActivationFunctionType as F
+
+BF, F32, I32, U16 = "bfloat16", "float32", "int32", "uint16"
+V = 2048
+SCRATCH = {
+    "dtx": ("dram", [8, 128, 32], I32), "drx": ("dram", [8, 128, 32], I32),
+    "dst": ("dram", [8, 128, 16], BF), "drs": ("dram", [8, 128, 16], BF),
+    "pmi": ("sbuf", [128, 128], I32), "eni": ("sbuf", [128, 128], I32),
+    "pmo": ("sbuf", [128, 128], U16), "eno": ("sbuf", [128, 128], U16),
+    "pmi2": ("sbuf", [128, 128], I32), "eni2": ("sbuf", [128, 128], I32),
+    "pmo2": ("sbuf", [128, 128], U16), "eno2": ("sbuf", [128, 128], U16),
+    "stm": ("sbuf", [128, V], BF), "stm2": ("sbuf", [128, V], BF),
+    "win": ("sbuf", [128, V], BF), "plc": ("sbuf", [128, V], BF),
+    "cls": ("sbuf", [128, V], BF), "ver": ("sbuf", [128, V], BF),
+    "red": ("sbuf", [128, 256], BF), "per": ("sbuf", [128, 144], BF),
+    "xs": ("sbuf", [128, 128], BF), "land": ("sbuf", [128, 128], BF),
+    "t64": ("sbuf", [128, 64], BF), "t32": ("sbuf", [128, 32], BF),
+    "ys": ("sbuf", [128, 16], BF), "land2": ("sbuf", [128, 128], BF),
+    "flg": ("sbuf", [128, 128], BF), "lnv": ("sbuf", [128, 128], F32),
+    "yi": ("sbuf", [128, 128], I32), "yf": ("sbuf", [128, 128], F32), "cf": ("sbuf", [128, 4], F32),
+    "ones": ("sbuf", [128, 128], BF), "ident": ("sbuf", [128, 128], BF), "sel": ("sbuf", [128, 8], BF),
+    "sel2": ("sbuf", [128, 16], BF), "msk": ("sbuf", [128, 256], BF), "ratio": ("sbuf", [128, 128], F32),
+    "enc": ("sbuf", [128, 128], BF), "c2": ("sbuf", [128, 4], F32), "lnc": ("sbuf", [128, 4], F32),
+    "acol": ("sbuf", [128, 4], F32), "hal": ("sbuf", [128, 4], F32), "big": ("sbuf", [128, 4], F32),
+    "bigb": ("sbuf", [128, 4], BF),
+    "pi": ("sbuf", [128, 10], I32), "pa": ("sbuf", [128, 10], I32), "pb": ("sbuf", [128, 10], I32),
+    "pc8": ("sbuf", [128, 10], I32), "pd": ("sbuf", [128, 10], I32), "pe16": ("sbuf", [128, 10], I32),
+    "pl": ("sbuf", [128, 10], U16),
+    "psA": ("psum", [128, 1024], BF), "psB": ("psum", [128, 1024], BF), "psC": ("psum", [128, 1024], BF),
+    "psD": ("psum", [128, 1024], BF), "psE": ("psum", [128, 1024], BF), "psX": ("psum", [128, 512], F32),
+    "psR": ("psum", [128, 512], F32), "psT": ("psum", [128, 512], F32),
+}
+SEMAPHORES = ("dpm den dtx down dlist dmask dy dcnt gd1 gd2 arrL arrS arrM arrY loc vones gident gsel gpi vstm vc2 sac "
+              "vrt vw0 vw1 vw2 vw3 sw3 vpm ven pe0 venc vmsk vrd0 vhal vbig vp1 vp3 vp4 vp5 szero vp2 vg sg0 sg1 sg2 sc0 "
+              "sc1 sc2 sc3 vm0 vm1 sm0 sm1 px vxs vown vt1 vt2 vred vper sper pwA pwB pwC pwD pwE wv ws vys vown2 pt sln "
+              "vyi vyf vflg pc scf").split()
+
+X0, X1, X2 = 704, 1216, 1728
+BANKS = [("B", 0, 1), ("A", 1, 1), ("D", 2, 2), ("C", 4, 2), ("E", 6, 2)]
+
+
+def rank_program(g, core, T, topo):
+    me = T.rank_of(core)
+    if me is None:
+        return
+    ve, se, pe, sy = g.vector, g.scalar, g.tensor, g.sync
+    n = {s: 0 for s in SEMAPHORES}
+
+    def inc(ins, name, k=1):
+        ins.then_inc(T.sem[name], k)
+        n[name] += k
+
+    def wait(queue, *names):
+        for s in names:
+            queue.wait_ge(T.sem[s], n[s])
+
+    others = [c for c in T.cores if c != core]
+    far = [c for c in others if topo.die(c) != topo.die(core)]
+    near = [c for c in others if topo.die(c) == topo.die(core)]
+    order = []
+    while far or near:
+        if far:
+            order.append(far.pop(0))
+        if near:
+            order.append(near.pop(0))
+
+    def send(src_of, dst, arr):
+        trs = []
+        for k, c in enumerate(order):
+            e = topo.engines(core, c)
+            m = (1 << e[k]) | (1 << e[k + len(e) // 2])
+            rid, pid, _s = topo.addr(c)
+            trs.append(RemoteDMATransfer(dst_ids=[DstId(rid=rid, pnc=pid)], dma_engine_mask=m, remote_sem=T.sem[arr],
+                                         src=src_of(T.rank_of(c)), dst=dst))
+            n["loc"] += 2
+            n[arr] += 2
+        g.remote_dma_fused(trs, local_sem=T.sem.loc)
+
+    inc(sy.dma_start(T.pmi[:], T.pm[:]), "dpm", 16)
+    inc(se.dma_start(T.eni[:], T.en[:]), "den", 16)
+    inc(sy.dma_start(T.dtx[:, 0:64, :], T.pm[:]), "dtx", 16)
+    inc(se.dma_start(T.dtx[:, 64:128, :], T.en[:]), "dtx", 16)
+    own = slice(16 * me, 16 * me + 16)
+    inc(sy.dma_start(T.drx[me, 0:64, :], T.pm[own, :]), "down", 16)
+    inc(sy.dma_start(T.drx[me, 64:128, :], T.en[own, :]), "down", 16)
+
+    inc(ve.memset(T.c2[:, 0:2], math.exp(16.0 / math.log(2.0))), "vc2")
+    inc(ve.memset(T.ones[:], 1.0), "vones")
+    inc(ve.memset(T.stm[:], 0.0), "vstm")
+    inc(ve.memset(T.ratio[:], 2.0 ** (1.0 / 32)), "vrt")
+
+    wait(g, "vones")
+    inc(g.affine_select(T.ident[:], T.ones[:], [[-1, 128]], A.is_equal, 0.0, 0, 1), "gident")
+    inc(g.affine_select(T.sel[:], T.ones[:, 0:8], [[-16, 8]], A.is_equal, 0.0, 0, 1), "gsel")
+    wait(g, "vstm")
+    inc(g.dma_start(T.stm[0:128:16, :], T.st[:]), "gd1", 16)
+    inc(g.dma_start(T.dst[:], T.st[:]), "gd2", 16)
+    inc(g.affine_select(T.sel2[:], T.ones[:, 0:16], [[-16, 8], [-1, 2]], A.is_equal, 0.0, 0, 1), "gsel")
+    inc(g.iota(T.pi[:], [[0, 10]], 0, 1), "gpi")
+
+    wait(se, "vc2")
+    inc(se.activation(T.lnc[:, 0:2], T.c2[:, 0:2], F.Ln, accum_out=T.acol[:, 0:1]), "sac")
+
+    wait(ve, "vrt")
+    inc(ve.tensor_tensor_scan(T.win[:, 0:128], T.ratio[:], T.ratio[:], 2.0 ** (-64 - 1.0 / 32), A.mult, A.min), "vw0")
+    wait(ve, "vw0")
+    inc(ve.tensor_scalar(T.win[:, 128:256], T.win[:, 0:128], 2.0 ** 4, None, A.mult), "vw1")
+    wait(ve, "vw1")
+    inc(ve.tensor_scalar(T.win[:, 256:512], T.win[:, 0:256], 2.0 ** 8, None, A.mult), "vw2")
+    wait(se, "vw2")
+    inc(se.activation(T.win[:, 1536:2048], T.win[:, 0:512], F.Copy, scale=2.0 ** 48), "sw3")
+    wait(ve, "vw2")
+    for k in (1, 2):
+        inc(ve.tensor_scalar(T.win[:, 512 * k:512 * k + 512], T.win[:, 0:512], 2.0 ** (16 * k), None, A.mult), "vw3")
+    wait(ve, "dpm")
+    inc(ve.tensor_copy(T.pmo[:], T.pmi[:]), "vpm")
+
+    wait(g, "dtx")
+    send(lambda r: T.dtx[r], T.drx[me], "arrL")
+    wait(g, "gd2")
+    send(lambda r: T.dst[r], T.drs[me], "arrS")
+    wait(sy, "gd2")
+    inc(sy.dma_start(T.drs[me], T.dst[me]), "down", 16)
+    wait(sy, "down", "arrL")
+    inc(sy.dma_start(T.pmi2[:], T.drx[:, 0:64, :]), "dlist", 16)
+    inc(sy.dma_start(T.eni2[:], T.drx[:, 64:128, :]), "dlist", 16)
+
+    wait(pe, "vw3", "vw2", "sw3", "gsel")
+    for b in range(16):
+        inc(pe.matmul(T.psT[:, b:128:16], T.win[:, 128 * b:128 * b + 128], T.sel[:], True, True), "pe0")
+
+    def phase(first, pmo, eno, stm, ready, turn, sel):
+        wait(ve, *ready)
+        inc(ve.tensor_copy(T.plc[:, 0:X0], T.win[:].indirect(pmo[:, 0:X0 // 16])), "vg")
+        wait(se, *ready)
+        cut = [X0, X1, X2, V]
+        for k in range(3):
+            a, b = cut[k], cut[k + 1]
+            inc(se.activation(T.plc[:, a:b], T.win[:].indirect(pmo[:, a // 16:b // 16]), F.Copy), "sg%d" % k)
+        if first:
+            wait(ve, "den")
+            inc(ve.tensor_copy(T.eno[:], T.eni[:]), "ven")
+            wait(ve, "gd1")
+        else:
+            wait(ve, "dmask")
+        lo = 0
+        for k, hi in enumerate(cut):
+            wait(ve, "vg" if k == 0 else "sg%d" % (k - 1))
+            if k:
+                wait(ve, "sc%d" % (k - 1))
+            inc(ve.tensor_tensor_scan(T.cls[:, lo:hi], stm[:, lo:hi], T.plc[:, lo:hi],
+                                      T.cls[:, lo - 1:lo] if k else 1.0, A.max, A.min), "sc%d" % k)
+            lo = hi
+        wait(ve, "sc3")
+        wait(se, "sc3")
+        if first:
+            wait(ve, "ven")
+            wait(se, "ven")
+        for k, a, b in ((0, 0, 768), (1, 768, 1024)):
+            inc(ve.tensor_copy(T.ver[:, a:b], T.cls[:].indirect(eno[:, a // 16:b // 16])), "vm%d" % k)
+            a, b = a + 1024, b + 1024
+            inc(se.activation(T.ver[:, a:b], T.cls[:].indirect(eno[:, a // 16:b // 16]), F.Copy), "sm%d" % k)
+        for s, b0, b1 in (("vm0", 0, 6), ("sm0", 8, 14), ("vm1", 6, 8), ("sm1", 14, 16)):
+            wait(pe, s)
+            for b in range(b0, b1):
+                inc(pe.matmul(turn(b), T.ver[:, 128 * b:128 * b + 128], sel, True, True), "px")
+
+    phase(True, T.pmo, T.eno, T.stm, ("vw3", "vw2", "sw3", "vpm"), lambda b: T.psX[:, b:128:16], T.sel[:])
+    inc(se.activation(T.stm2[:], T.stm[:], F.Copy, scale=0.0), "szero")
+    wait(sy, "szero", "arrS", "down")
+    for k in (0, 1):
+        inc(sy.dma_start(T.stm2[k:128:16, :], T.drs[0:8]), "dmask", 16)
+    wait(ve, "px")
+    inc(ve.tensor_copy(T.xs[:], T.psX[:, 0:128]), "vxs")
+    wait(g, "vxs")
+    mine = slice(16 * me, 16 * me + 16)
+    send(lambda r: T.xs[:, 16 * r:16 * r + 16], T.land[:, mine], "arrM")
+    wait(ve, "vxs")
+    inc(ve.tensor_copy(T.land[:, mine], T.xs[:, mine]), "vown")
+    inc(ve.memset(T.msk[:], 0.0), "vmsk")
+    inc(ve.memset(T.red[:], 1.0), "vrd0")
+    wait(ve, "vmsk")
+    inc(ve.memset(T.msk[:, 0:256:16], 1.0), "vmsk")
+    wait(ve, "gsel")
+    for k in (0, 1):
+        inc(ve.tensor_reduce(T.hal[:, k:k + 1], T.sel2[:, k:16:2], AxisListType.X, A.max), "vhal")
+    wait(ve, "vhal")
+    inc(ve.tensor_scalar(T.big[:, 0:2], T.hal[:, 0:2], -1.0, 1.0, A.mult, A.add), "vbig")
+    inc(ve.tensor_scalar(T.bigb[:, 0:2], T.hal[:, 0:2], -1.0, 1.0, A.mult, A.add), "vbig")
+    wait(ve, "gpi")
+    inc(ve.tensor_scalar(T.pa[:], T.pi[:], 14, None, A.bitwise_and), "vp1")
+    inc(ve.tensor_scalar(T.pb[:], T.pi[:], 1, None, A.bitwise_and), "vp1")
+    wait(ve, "vp1")
+    inc(ve.tensor_scalar(T.pc8[:], T.pa[:], 8, 15, A.mult, A.add), "vp3")
+    inc(ve.tensor_scalar(T.pd[:], T.pb[:], 128, None, A.mult), "vp3")
+    wait(ve, "vp3")
+    inc(ve.tensor_tensor(T.pe16[:], T.pc8[:], T.pd[:], A.add), "vp4")
+    wait(ve, "vp4")
+    inc(ve.tensor_copy(T.pl[:], T.pe16[:]), "vp5")
+    wait(ve, "dlist")
+    inc(ve.tensor_copy(T.pmo2[:], T.pmi2[:]), "vp2")
+    inc(ve.tensor_copy(T.eno2[:], T.eni2[:]), "vp2")
+    wait(ve, "pe0")
+    inc(ve.tensor_copy(T.enc[:], T.psT[:, 0:128]), "venc")
+    wait(ve, "arrM", "vown")
+    inc(ve.tensor_tensor(T.t64[:], T.land[:, 0:64], T.land[:, 64:128], A.min), "vt1")
+    wait(ve, "vt1")
+    inc(ve.tensor_tensor(T.t32[:], T.t64[:, 0:32], T.t64[:, 32:64], A.min), "vt2")
+    wait(ve, "vt2", "vrd0")
+    inc(ve.tensor_tensor(T.red[:, 15:256:16], T.t32[:, 0:16], T.t32[:, 16:32], A.min), "vred")
+
+    for h in (2, 3, 4):
+        wait(ve, "vred", "vp5")
+        inc(ve.tensor_copy(T.per[:, 0:96], T.red[:].indirect(T.pl[:, 0:6])), "vper")
+        wait(se, "vred", "vp5")
+        inc(se.activation(T.per[:, 96:144], T.red[:].indirect(T.pl[:, 6:9]), F.Copy), "sper")
+        wait(pe, "vper", "sper", "gident")
+        for name, b0, k in BANKS:
+            for j in range(k):
+                b = b0 + j
+                inc(pe.transpose(T["ps" + name][:, 128 * j:128 * j + 128], T.per[:, 2 * b:2 * b + 128], T.ident[:]),
+                    "pw" + name)
+        for name, b0, k in BANKS:
+            src, lo, hi = T["ps" + name][:, 0:128 * k], 128 * b0, 128 * (b0 + k)
+            for half in (0, 1):
+                dst = T.win[:, 1024 * half + lo:1024 * half + hi]
+                if name in "ACE":
+                    wait(ve, "pw" + name, "vbig")
+                    inc(ve.tensor_scalar(dst, src, T.bigb[:, half:half + 1], None, A.max), "wv")
+                else:
+                    wait(se, "pw" + name, "vbig")
+                    inc(se.activation(dst, src, F.Identity, bias=T.big[:, half:half + 1],
+                                      scale=T.hal[:, half:half + 1]), "ws")
+        phase(False, T.pmo2, T.eno2, T.stm2, ("wv", "ws", "vp2"), lambda b: T.psX[:, 16 * b:16 * b + 16], T.sel2[:])
+        wait(ve, "px", "vmsk")
+        inc(ve.tensor_tensor_scan(T.red[:], T.msk[:], T.psX[:, 0:256], 1.0, A.max, A.min), "vred")
+
+    wait(ve, "vred")
+    inc(ve.tensor_copy(T.ys[:], T.red[:, 15:256:16]), "vys")
+    wait(g, "vys")
+    send(lambda r: T.ys[:], T.land2[:, mine], "arrY")
+    wait(ve, "vys")
+    inc(ve.tensor_copy(T.land2[:, mine], T.ys[:]), "vown2")
+    wait(pe, "arrY", "vown2")
+    inc(pe.matmul(T.psT[:, 0:128], T.land2[:], T.ident[:], True, True), "pt")
+    wait(ve, "arrY", "vown2", "venc")
+    inc(ve.tensor_tensor(T.flg[:], T.land2[:], T.enc[:], A.is_equal), "vflg")
+    wait(se, "pt")
+    inc(se.activation(T.lnv[:], T.psT[:, 0:128], F.Ln, scale=2.0 ** 32), "sln")
+    wait(ve, "sln", "sac")
+    inc(ve.tensor_scalar(T.yi[:], T.lnv[:], T.acol[:, 0:1], 1024.0, A.mult, A.add), "vyi")
+    wait(ve, "vyi")
+    inc(ve.tensor_copy(T.yf[:], T.yi[:]), "vyf")
+    wait(sy, "vyf")
+    inc(sy.dma_start(T.y[:], T.yf[:]), "dy", 16)
+    wait(pe, "vflg", "vones")
+    for b in range(16):
+        pc = pe.matmul(T.psR[0:8, 0:1], T.flg[:, b:128:16], T.ones[:, 0:1], b == 0, b == 15)
+    inc(pc, "pc")
+    wait(se, "pc")
+    inc(se.activation(T.cf[0:8, 0:1], T.psR[0:8, 0:1], F.Copy), "scf")
+    wait(se, "scf")
+    inc(se.dma_start(T.cnt[:], T.cf[0:8, 0:1]), "dcnt", 16)
+    wait(sy, "dy")
+    wait(se, "dcnt")
+    wait(g, "loc")

@@ -11,34 +11,41 @@ SCRATCH = {
     "pmo": ("sbuf", [128, 128], U16), "eno": ("sbuf", [128, 128], U16),
     "pmi2": ("sbuf", [128, 128], I32), "eni2": ("sbuf", [128, 128], I32),
     "pmo2": ("sbuf", [128, 128], U16), "eno2": ("sbuf", [128, 128], U16),
-    "stm": ("sbuf", [128, V], BF), "stm2": ("sbuf", [128, V], BF),
+    "stm": ("sbuf", [128, V], BF),
     "win": ("sbuf", [128, V], BF), "plc": ("sbuf", [128, V], BF),
     "cls": ("sbuf", [128, V], BF), "ver": ("sbuf", [128, V], BF),
-    "red": ("sbuf", [128, 256], BF), "per": ("sbuf", [128, 144], BF),
-    "xs": ("sbuf", [128, 128], BF), "land": ("sbuf", [128, 128], BF),
-    "t64": ("sbuf", [128, 64], BF), "t32": ("sbuf", [128, 32], BF),
+    "rep": ("sbuf", [128, 3072], BF), "red": ("sbuf", [128, 256], BF),
+    "xs": ("sbuf", [128, 128], BF), "land": ("sbuf", [128, 128], BF), "lr": ("sbuf", [128, 256], BF),
     "ys": ("sbuf", [128, 16], BF), "land2": ("sbuf", [128, 128], BF),
     "flg": ("sbuf", [128, 128], BF), "lnv": ("sbuf", [128, 128], F32),
     "yi": ("sbuf", [128, 128], I32), "yf": ("sbuf", [128, 128], F32), "cf": ("sbuf", [128, 4], F32),
-    "ones": ("sbuf", [128, 128], BF), "ident": ("sbuf", [128, 128], BF), "sel": ("sbuf", [128, 8], BF),
-    "sel2": ("sbuf", [128, 16], BF), "msk": ("sbuf", [128, 256], BF), "ratio": ("sbuf", [128, 128], F32),
+    "ones": ("sbuf", [128, 192], BF), "ident": ("sbuf", [128, 128], BF), "sel": ("sbuf", [128, 32], BF),
+    "m16": ("sbuf", [128, 192], BF), "m24": ("sbuf", [128, 192], BF), "ratio": ("sbuf", [128, 128], F32),
     "enc": ("sbuf", [128, 128], BF), "c2": ("sbuf", [128, 4], F32), "lnc": ("sbuf", [128, 4], F32),
-    "acol": ("sbuf", [128, 4], F32), "hal": ("sbuf", [128, 4], F32), "big": ("sbuf", [128, 4], F32),
-    "bigb": ("sbuf", [128, 4], BF),
-    "pi": ("sbuf", [128, 10], I32), "pa": ("sbuf", [128, 10], I32), "pb": ("sbuf", [128, 10], I32),
-    "pc8": ("sbuf", [128, 10], I32), "pd": ("sbuf", [128, 10], I32), "pe16": ("sbuf", [128, 10], I32),
-    "pl": ("sbuf", [128, 10], U16),
-    "psA": ("psum", [128, 1024], BF), "psB": ("psum", [128, 1024], BF), "psC": ("psum", [128, 1024], BF),
-    "psD": ("psum", [128, 1024], BF), "psE": ("psum", [128, 1024], BF), "psX": ("psum", [128, 512], F32),
-    "psR": ("psum", [128, 512], F32), "psT": ("psum", [128, 512], F32),
+    "acol": ("sbuf", [128, 4], F32), "hal": ("sbuf", [128, 8], BF),
+    "pi": ("sbuf", [128, 16], I32), "pa": ("sbuf", [128, 16], I32), "pl": ("sbuf", [128, 16], U16),
+    "t0": ("psum", [128, 512], F32), "t1": ("psum", [128, 512], F32), "t2": ("psum", [128, 512], F32),
+    "t3": ("psum", [128, 512], F32),
+    "w0": ("psum", [128, 1024], BF), "w1": ("psum", [128, 1024], BF), "w2": ("psum", [128, 1024], BF),
+    "w3": ("psum", [128, 1024], BF),
 }
 SEMAPHORES = ("dpm den dtx down dlist dmask dy dcnt gd1 gd2 arrL arrS arrM arrY loc vones gident gsel gpi vstm vc2 sac "
-              "vrt vw0 vw1 vw2 vw3 sw3 vpm ven pe0 venc vmsk vrd0 vhal vbig vp1 vp3 vp4 vp5 szero vp2 vg sg0 sg1 sg2 sc0 "
-              "sc1 sc2 sc3 vm0 vm1 sm0 sm1 px vxs vown vt1 vt2 vred vper sper pwA pwB pwC pwD pwE wv ws vys vown2 pt sln "
-              "vyi vyf vflg pc scf").split()
+              "vrt vw0 sw1 sw2 sw3 vw4 sw4 vpm ven pe0 venc g16 g24 vrep srep vhal vp1 vp5 vp2 pg0 pg1 pg2 pg3 sc0 "
+              "sc1 sc2 sc3 eg0 eg1 eg2 eg3 eg4 eg5 eg6 eg7 pm0 pm1 pm2 pm3 mn0 mn1 mn2 mn3 pw0 pw1 pw2 pw3 wv ws vxs vown "
+              "vl sl vys vown2 pt sln vyi vyf vflg pc scf").split()
 
-X0, X1, X2 = 704, 1216, 1728
-BANKS = [("B", 0, 1), ("A", 1, 1), ("D", 2, 2), ("C", 4, 2), ("E", 6, 2)]
+PCUT = [("v", 768), ("s", 1536), ("s", 2048)]
+PV = ["g0", "c1", "c2"]
+EG = [("s", 0, 4), ("v", 8, 12), ("s", 4, 7), ("s", 7, 8), ("v", 12, 16)]
+SETS = [(0, 4), (8, 12), (4, 8), (12, 16)]
+BANKS = [("s", 0, 1), ("v", 1, 4), ("v", 4, 6), ("s", 6, 8)]
+EV = ["g1", "g4", "m1", "m0", "m3", "m2", "w1", "w2"]
+ES = ["g0", "g2", "g3", "w0", "w3"]
+EP = ["g0", "g1", "g2", "g4", "g3", "w0", "w1", "w3", "w2"]
+XBANKS = [("s", 0, 1), ("v", 1, 3), ("s", 3, 5), ("v", 5, 8)]
+FG = [("v", 0, 6), ("s", 8, 14), ("v", 6, 8), ("s", 14, 16)]
+LG = [("v", 0, 6), ("s", 6, 12), ("v", 12, 14), ("s", 14, 16)]
+LSETS = [(0, 12), (12, 14), (14, 16)]
 
 
 def rank_program(g, core, T, topo):
@@ -46,15 +53,19 @@ def rank_program(g, core, T, topo):
     if me is None:
         return
     ve, se, pe, sy = g.vector, g.scalar, g.tensor, g.sync
+    Q = {"v": ve, "s": se, "p": pe, "y": sy, "g": g}
     n = {s: 0 for s in SEMAPHORES}
+    seen = {}
 
     def inc(ins, name, k=1):
         ins.then_inc(T.sem[name], k)
         n[name] += k
 
-    def wait(queue, *names):
+    def wait(q, *names):
         for s in names:
-            queue.wait_ge(T.sem[s], n[s])
+            if seen.get((q, s), 0) < n[s]:
+                Q[q].wait_ge(T.sem[s], n[s])
+                seen[(q, s)] = n[s]
 
     others = [c for c in T.cores if c != core]
     far = [c for c in others if topo.die(c) != topo.die(core)]
@@ -66,203 +77,272 @@ def rank_program(g, core, T, topo):
         if near:
             order.append(near.pop(0))
 
+    def did(c):
+        rid, pid, _s = topo.addr(c)
+        return DstId(rid=rid, pnc=pid)
+
     def send(src_of, dst, arr):
         trs = []
         for k, c in enumerate(order):
             e = topo.engines(core, c)
             m = (1 << e[k]) | (1 << e[k + len(e) // 2])
-            rid, pid, _s = topo.addr(c)
-            trs.append(RemoteDMATransfer(dst_ids=[DstId(rid=rid, pnc=pid)], dma_engine_mask=m, remote_sem=T.sem[arr],
+            trs.append(RemoteDMATransfer(dst_ids=[did(c)], dma_engine_mask=m, remote_sem=T.sem[arr],
                                          src=src_of(T.rank_of(c)), dst=dst))
             n["loc"] += 2
             n[arr] += 2
         g.remote_dma_fused(trs, local_sem=T.sem.loc)
 
+    def gather(q, out, win, off, name):
+        if q == "v":
+            inc(ve.tensor_copy(out, win.indirect(off)), name)
+        else:
+            inc(se.activation(out, win.indirect(off), F.Copy), name)
+
     inc(sy.dma_start(T.pmi[:], T.pm[:]), "dpm", 16)
-    inc(se.dma_start(T.eni[:], T.en[:]), "den", 16)
+    inc(ve.memset(T.ratio[:], 2.0 ** (1.0 / 32)), "vrt")
+    wait("v", "vrt")
+    inc(ve.tensor_tensor_scan(T.win[:, 0:128], T.ratio[:], T.ratio[:], 2.0 ** (-64 - 1.0 / 32), A.mult, A.min), "vw0")
+    inc(ve.memset(T.stm[:], 0.0), "vstm")
+    inc(ve.memset(T.ones[:], 1.0), "vones")
+    inc(ve.memset(T.c2[:, 0:2], math.exp(16.0 / math.log(2.0))), "vc2")
+    for k, (a, b) in enumerate((("vw0", "sw1"), ("sw1", "sw2"), ("sw2", "sw3"))):
+        w = 128 << k
+        wait("s", a)
+        inc(se.activation(T.win[:, w:2 * w], T.win[:, 0:w], F.Copy, scale=2.0 ** (w // 32)), b)
+    wait("s", "sw3")
+    inc(se.activation(T.win[:, 1728:2048], T.win[:, 704:1024], F.Copy, scale=2.0 ** 32), "sw4")
+    wait("v", "dpm")
+    inc(ve.tensor_copy(T.pmo[:], T.pmi[:]), "vpm")
+    wait("v", "sw3")
+    inc(ve.tensor_scalar(T.win[:, 1024:1728], T.win[:, 0:704], 2.0 ** 32, None, A.mult), "vw4")
+
+    wait("g", "vstm")
+    inc(g.dma_start(T.stm[0:128:16, :], T.st[:]), "gd1", 16)
+    inc(g.dma_start(T.dst[:], T.st[:]), "gd2", 16)
+    wait("g", "vones")
+    inc(g.affine_select(T.sel[:], T.ones[:, 0:32], [[0, 2], [-8, 16]], A.is_equal, 0.0, 0, 1), "gsel")
+    inc(g.affine_select(T.ident[:], T.ones[:, 0:128], [[-1, 128]], A.is_equal, 0.0, 0, 1), "gident")
+    inc(g.iota(T.pi[:], [[1, 16]], 0, 16), "gpi")
+    sel8 = T.sel[:, 0:16:2]
+
+    wait("y", "dpm")
+    inc(sy.dma_start(T.eni[:], T.en[:]), "den", 16)
     inc(sy.dma_start(T.dtx[:, 0:64, :], T.pm[:]), "dtx", 16)
-    inc(se.dma_start(T.dtx[:, 64:128, :], T.en[:]), "dtx", 16)
+    inc(sy.dma_start(T.dtx[:, 64:128, :], T.en[:]), "dtx", 16)
     own = slice(16 * me, 16 * me + 16)
     inc(sy.dma_start(T.drx[me, 0:64, :], T.pm[own, :]), "down", 16)
     inc(sy.dma_start(T.drx[me, 64:128, :], T.en[own, :]), "down", 16)
 
-    inc(ve.memset(T.c2[:, 0:2], math.exp(16.0 / math.log(2.0))), "vc2")
-    inc(ve.memset(T.ones[:], 1.0), "vones")
-    inc(ve.memset(T.stm[:], 0.0), "vstm")
-    inc(ve.memset(T.ratio[:], 2.0 ** (1.0 / 32)), "vrt")
-
-    wait(g, "vones")
-    inc(g.affine_select(T.ident[:], T.ones[:], [[-1, 128]], A.is_equal, 0.0, 0, 1), "gident")
-    inc(g.affine_select(T.sel[:], T.ones[:, 0:8], [[-16, 8]], A.is_equal, 0.0, 0, 1), "gsel")
-    wait(g, "vstm")
-    inc(g.dma_start(T.stm[0:128:16, :], T.st[:]), "gd1", 16)
-    inc(g.dma_start(T.dst[:], T.st[:]), "gd2", 16)
-    inc(g.affine_select(T.sel2[:], T.ones[:, 0:16], [[-16, 8], [-1, 2]], A.is_equal, 0.0, 0, 1), "gsel")
-    inc(g.iota(T.pi[:], [[0, 10]], 0, 1), "gpi")
-
-    wait(se, "vc2")
-    inc(se.activation(T.lnc[:, 0:2], T.c2[:, 0:2], F.Ln, accum_out=T.acol[:, 0:1]), "sac")
-
-    wait(ve, "vrt")
-    inc(ve.tensor_tensor_scan(T.win[:, 0:128], T.ratio[:], T.ratio[:], 2.0 ** (-64 - 1.0 / 32), A.mult, A.min), "vw0")
-    wait(ve, "vw0")
-    inc(ve.tensor_scalar(T.win[:, 128:256], T.win[:, 0:128], 2.0 ** 4, None, A.mult), "vw1")
-    wait(ve, "vw1")
-    inc(ve.tensor_scalar(T.win[:, 256:512], T.win[:, 0:256], 2.0 ** 8, None, A.mult), "vw2")
-    wait(se, "vw2")
-    inc(se.activation(T.win[:, 1536:2048], T.win[:, 0:512], F.Copy, scale=2.0 ** 48), "sw3")
-    wait(ve, "vw2")
-    for k in (1, 2):
-        inc(ve.tensor_scalar(T.win[:, 512 * k:512 * k + 512], T.win[:, 0:512], 2.0 ** (16 * k), None, A.mult), "vw3")
-    wait(ve, "dpm")
-    inc(ve.tensor_copy(T.pmo[:], T.pmi[:]), "vpm")
-
-    wait(g, "dtx")
+    wait("g", "dtx")
     send(lambda r: T.dtx[r], T.drx[me], "arrL")
-    wait(g, "gd2")
+    wait("g", "gd2")
     send(lambda r: T.dst[r], T.drs[me], "arrS")
-    wait(sy, "gd2")
+    wait("y", "gd2")
     inc(sy.dma_start(T.drs[me], T.dst[me]), "down", 16)
-    wait(sy, "down", "arrL")
+    wait("y", "down", "arrL")
     inc(sy.dma_start(T.pmi2[:], T.drx[:, 0:64, :]), "dlist", 16)
     inc(sy.dma_start(T.eni2[:], T.drx[:, 64:128, :]), "dlist", 16)
 
-    wait(pe, "vw3", "vw2", "sw3", "gsel")
+    wait("p", "vw4", "sw4", "gsel")
     for b in range(16):
-        inc(pe.matmul(T.psT[:, b:128:16], T.win[:, 128 * b:128 * b + 128], T.sel[:], True, True), "pe0")
+        inc(pe.matmul(T.t1[:, b:128:16], T.win[:, 128 * b:128 * b + 128], sel8, True, True), "pe0")
 
-    def phase(first, pmo, eno, stm, ready, turn, sel):
-        wait(ve, *ready)
-        inc(ve.tensor_copy(T.plc[:, 0:X0], T.win[:].indirect(pmo[:, 0:X0 // 16])), "vg")
-        wait(se, *ready)
-        cut = [X0, X1, X2, V]
-        for k in range(3):
-            a, b = cut[k], cut[k + 1]
-            inc(se.activation(T.plc[:, a:b], T.win[:].indirect(pmo[:, a // 16:b // 16]), F.Copy), "sg%d" % k)
-        if first:
-            wait(ve, "den")
-            inc(ve.tensor_copy(T.eno[:], T.eni[:]), "ven")
-            wait(ve, "gd1")
-        else:
-            wait(ve, "dmask")
-        lo = 0
-        for k, hi in enumerate(cut):
-            wait(ve, "vg" if k == 0 else "sg%d" % (k - 1))
-            if k:
-                wait(ve, "sc%d" % (k - 1))
-            inc(ve.tensor_tensor_scan(T.cls[:, lo:hi], stm[:, lo:hi], T.plc[:, lo:hi],
-                                      T.cls[:, lo - 1:lo] if k else 1.0, A.max, A.min), "sc%d" % k)
-            lo = hi
-        wait(ve, "sc3")
-        wait(se, "sc3")
-        if first:
-            wait(ve, "ven")
-            wait(se, "ven")
-        for k, a, b in ((0, 0, 768), (1, 768, 1024)):
-            inc(ve.tensor_copy(T.ver[:, a:b], T.cls[:].indirect(eno[:, a // 16:b // 16])), "vm%d" % k)
-            a, b = a + 1024, b + 1024
-            inc(se.activation(T.ver[:, a:b], T.cls[:].indirect(eno[:, a // 16:b // 16]), F.Copy), "sm%d" % k)
-        for s, b0, b1 in (("vm0", 0, 6), ("sm0", 8, 14), ("vm1", 6, 8), ("sm1", 14, 16)):
-            wait(pe, s)
-            for b in range(b0, b1):
-                inc(pe.matmul(turn(b), T.ver[:, 128 * b:128 * b + 128], sel, True, True), "px")
+    def places(first, pmo, ready):
+        wait("v", *ready)
+        wait("s", *ready)
+        lo = [0] + [e for _q, e in PCUT]
 
-    phase(True, T.pmo, T.eno, T.stm, ("vw3", "vw2", "sw3", "vpm"), lambda b: T.psX[:, b:128:16], T.sel[:])
-    inc(se.activation(T.stm2[:], T.stm[:], F.Copy, scale=0.0), "szero")
-    wait(sy, "szero", "arrS", "down")
-    for k in (0, 1):
-        inc(sy.dma_start(T.stm2[k:128:16, :], T.drs[0:8]), "dmask", 16)
-    wait(ve, "px")
-    inc(ve.tensor_copy(T.xs[:], T.psX[:, 0:128]), "vxs")
-    wait(g, "vxs")
+        def piece(k):
+            a, b = lo[k], lo[k + 1]
+            gather(PCUT[k][0], T.plc[:, a:b], T.win[:], pmo[:, a // 16:b // 16], "pg%d" % k)
+        for k in range(len(PCUT)):
+            if PCUT[k][0] == "s":
+                piece(k)
+        done, scans = 0, 0
+        for op in PV:
+            k = int(op[1])
+            if op[0] == "g":
+                piece(k)
+                continue
+            if first and not scans:
+                wait("v", "den")
+                inc(ve.tensor_copy(T.eno[:], T.eni[:]), "ven")
+            wait("v", "gd1" if first else "dmask", *["pg%d" % j for j in range(done, k + 1)])
+            a, b = lo[done], lo[k + 1]
+            if scans:
+                wait("v", "sc%d" % (scans - 1))
+            inc(ve.tensor_tensor_scan(T.cls[:, a:b], T.stm[:, a:b], T.plc[:, a:b],
+                                      T.cls[:, a - 1:a] if scans else 1.0, A.max, A.min), "sc%d" % scans)
+            done, scans = k + 1, scans + 1
+        for q in "vs":
+            wait(q, "sc%d" % (scans - 1), "ven")
+        return "sc%d" % (scans - 1)
+
+    def vertices(pieces, k, eno):
+        q, b0, b1 = pieces[k]
+        gather(q, T.ver[:, 128 * b0:128 * b1], T.cls[:], eno[:, 8 * b0:8 * b1], "eg%d" % k)
+
+    def set_of(sets, b):
+        return [s for s, (b0, b1) in enumerate(sets) if b0 <= b < b1][0]
+
+    def spread(banks, k, step, *ready):
+        _q, b0, b1 = banks[k]
+        wait("p", "gident", *ready)
+        for b in range(b0, b1):
+            inc(pe.transpose(T["w%d" % k][:, 128 * (b - b0):128 * (b - b0 + 1)],
+                             T.rep[:, step * b + 256:step * b + 384], T.ident[:]), "pw%d" % k)
+
+    def window(banks, k):
+        q, b0, b1 = banks[k]
+        src = T["w%d" % k][:, 0:128 * (b1 - b0)]
+        wait(q, "pw%d" % k, "vhal")
+        for h in (0, 1):
+            dst, blank = T.win[:, 1024 * h + 128 * b0:1024 * h + 128 * b1], T.hal[:, 1 - h:2 - h]
+            if q == "v":
+                inc(ve.tensor_scalar(dst, src, blank, None, A.max), "wv")
+            else:
+                inc(se.activation(dst, src, F.Identity, bias=blank), "ws")
+
+    scanned = places(True, T.pmo, ("vw4", "sw4", "vpm"))
+    wait("y", scanned, "arrS", "down")
+    for h in (0, 8):
+        inc(sy.dma_start(T.stm[h:128:16, :], T.drs[0:8]), "dmask", 16)
+    for k in range(len(FG)):
+        vertices(FG, k, T.eno)
+    for k, (_q, b0, b1) in enumerate(FG):
+        wait("p", "eg%d" % k)
+        for b in range(b0, b1):
+            inc(pe.matmul(T.t0[:, b:128:16], T.ver[:, 128 * b:128 * b + 128], sel8, True, True), "pm0")
+    wait("v", "pm0")
+    inc(ve.tensor_copy(T.xs[:], T.t0[:, 0:128]), "vxs")
+    wait("g", "vxs")
     mine = slice(16 * me, 16 * me + 16)
     send(lambda r: T.xs[:, 16 * r:16 * r + 16], T.land[:, mine], "arrM")
-    wait(ve, "vxs")
+    wait("v", "vxs")
     inc(ve.tensor_copy(T.land[:, mine], T.xs[:, mine]), "vown")
-    inc(ve.memset(T.msk[:], 0.0), "vmsk")
-    inc(ve.memset(T.red[:], 1.0), "vrd0")
-    wait(ve, "vmsk")
-    inc(ve.memset(T.msk[:, 0:256:16], 1.0), "vmsk")
-    wait(ve, "gsel")
-    for k in (0, 1):
-        inc(ve.tensor_reduce(T.hal[:, k:k + 1], T.sel2[:, k:16:2], AxisListType.X, A.max), "vhal")
-    wait(ve, "vhal")
-    inc(ve.tensor_scalar(T.big[:, 0:2], T.hal[:, 0:2], -1.0, 1.0, A.mult, A.add), "vbig")
-    inc(ve.tensor_scalar(T.bigb[:, 0:2], T.hal[:, 0:2], -1.0, 1.0, A.mult, A.add), "vbig")
-    wait(ve, "gpi")
-    inc(ve.tensor_scalar(T.pa[:], T.pi[:], 14, None, A.bitwise_and), "vp1")
-    inc(ve.tensor_scalar(T.pb[:], T.pi[:], 1, None, A.bitwise_and), "vp1")
-    wait(ve, "vp1")
-    inc(ve.tensor_scalar(T.pc8[:], T.pa[:], 8, 15, A.mult, A.add), "vp3")
-    inc(ve.tensor_scalar(T.pd[:], T.pb[:], 128, None, A.mult), "vp3")
-    wait(ve, "vp3")
-    inc(ve.tensor_tensor(T.pe16[:], T.pc8[:], T.pd[:], A.add), "vp4")
-    wait(ve, "vp4")
-    inc(ve.tensor_copy(T.pl[:], T.pe16[:]), "vp5")
-    wait(ve, "dlist")
+    wait("s", "vc2")
+    inc(se.activation(T.lnc[:, 0:2], T.c2[:, 0:2], F.Ln, accum_out=T.acol[:, 0:1]), "sac")
+    inc(g.affine_select(T.m16[:], T.ones[:], [[0, 12], [1, 16]], A.is_equal, 0.0, 0, 0), "g16")
+    inc(g.affine_select(T.m24[:], T.ones[:], [[0, 8], [1, 24]], A.is_equal, 0.0, 0, 0), "g24")
+    inc(ve.memset(T.rep[:, 256:2304], 1.0), "vrep")
+    wait("s", "vones")
+    for b in (6, 7):
+        inc(se.activation(T.rep[:, 384 * b + 256:384 * b + 384], T.ones[:, 0:128], F.Copy), "srep")
+    wait("v", "gpi", "gsel")
+    inc(ve.tensor_scalar(T.pa[:], T.pi[:], 127, None, A.bitwise_and), "vp1")
+    for h in (0, 1):
+        inc(ve.tensor_reduce(T.hal[:, h:h + 1], T.sel[:, h:16:2], AxisListType.X, A.max), "vhal")
+    wait("v", "vp1")
+    inc(ve.tensor_copy(T.pl[:], T.pa[:]), "vp5")
+    wait("v", "dlist")
     inc(ve.tensor_copy(T.pmo2[:], T.pmi2[:]), "vp2")
     inc(ve.tensor_copy(T.eno2[:], T.eni2[:]), "vp2")
-    wait(ve, "pe0")
-    inc(ve.tensor_copy(T.enc[:], T.psT[:, 0:128]), "venc")
-    wait(ve, "arrM", "vown")
-    inc(ve.tensor_tensor(T.t64[:], T.land[:, 0:64], T.land[:, 64:128], A.min), "vt1")
-    wait(ve, "vt1")
-    inc(ve.tensor_tensor(T.t32[:], T.t64[:, 0:32], T.t64[:, 32:64], A.min), "vt2")
-    wait(ve, "vt2", "vrd0")
-    inc(ve.tensor_tensor(T.red[:, 15:256:16], T.t32[:, 0:16], T.t32[:, 16:32], A.min), "vred")
+    wait("s", "pe0")
+    inc(se.activation(T.enc[:], T.t1[:, 0:128], F.Copy), "venc")
+    for h, q in enumerate("vs"):
+        wait(q, "arrM", "vown", "vp5")
+        gather(q, T.lr[:, 128 * h:128 * h + 128], T.land[:], T.pl[:, 8 * h:8 * h + 8], q + "l")
+    for h, q in enumerate("vs"):
+        wait("v", q + "l", "g16", "vrep")
+        inc(ve.tensor_tensor_scan(T.rep[:, 128 + 8 * h:2176:16], T.m16[:, 0:128], T.lr[:, 128 * h:128 * h + 128],
+                                  1.0, A.max, A.min), "mn%d" % h)
+    for k in range(len(XBANKS)):
+        spread(XBANKS, k, 256, "mn0", "mn1")
+    for k in range(len(XBANKS)):
+        window(XBANKS, k)
 
-    for h in (2, 3, 4):
-        wait(ve, "vred", "vp5")
-        inc(ve.tensor_copy(T.per[:, 0:96], T.red[:].indirect(T.pl[:, 0:6])), "vper")
-        wait(se, "vred", "vp5")
-        inc(se.activation(T.per[:, 96:144], T.red[:].indirect(T.pl[:, 6:9]), F.Copy), "sper")
-        wait(pe, "vper", "sper", "gident")
-        for name, b0, k in BANKS:
-            for j in range(k):
-                b = b0 + j
-                inc(pe.transpose(T["ps" + name][:, 128 * j:128 * j + 128], T.per[:, 2 * b:2 * b + 128], T.ident[:]),
-                    "pw" + name)
-        for name, b0, k in BANKS:
-            src, lo, hi = T["ps" + name][:, 0:128 * k], 128 * b0, 128 * (b0 + k)
-            for half in (0, 1):
-                dst = T.win[:, 1024 * half + lo:1024 * half + hi]
-                if name in "ACE":
-                    wait(ve, "pw" + name, "vbig")
-                    inc(ve.tensor_scalar(dst, src, T.bigb[:, half:half + 1], None, A.max), "wv")
-                else:
-                    wait(se, "pw" + name, "vbig")
-                    inc(se.activation(dst, src, F.Identity, bias=T.big[:, half:half + 1],
-                                      scale=T.hal[:, half:half + 1]), "ws")
-        phase(False, T.pmo2, T.eno2, T.stm2, ("wv", "ws", "vp2"), lambda b: T.psX[:, 16 * b:16 * b + 16], T.sel2[:])
-        wait(ve, "px", "vmsk")
-        inc(ve.tensor_tensor_scan(T.red[:], T.msk[:], T.psX[:, 0:256], 1.0, A.max, A.min), "vred")
+    def turn(pieces, k, sets, wide):
+        _q, b0, b1 = pieces[k]
+        s = set_of(sets, b0)
+        wait("p", "eg%d" % k, "venc")
+        for b in range(b0, b1):
+            c = wide * (b - sets[s][0])
+            inc(pe.matmul(T["t%d" % s][:, c:c + wide], T.ver[:, 128 * b:128 * b + 128], T.sel[:, 0:wide], True, True),
+                "pm%d" % s)
 
-    wait(ve, "vred")
-    inc(ve.tensor_copy(T.ys[:], T.red[:, 15:256:16]), "vys")
-    wait(g, "vys")
-    send(lambda r: T.ys[:], T.land2[:, mine], "arrY")
-    wait(ve, "vys")
+    for _hop in (2, 3):
+        places(False, T.pmo2, ("wv", "ws", "vp2"))
+        todo = {"v": list(EV), "s": list(ES), "p": list(EP)}
+        made = set()
+        while todo["v"] or todo["s"] or todo["p"]:
+            for q in "vsp":
+                while todo[q]:
+                    op = todo[q][0]
+                    k = int(op[1])
+                    if q == "p" and op[0] == "w":
+                        need = ["m%d" % set_of(SETS, BANKS[k][1] + h) for h in (0, 8)]
+                    elif q == "p":
+                        need = [op]
+                    elif op[0] == "m":
+                        need = ["pg%d" % j for j in range(len(EG)) if set_of(SETS, EG[j][1]) == k]
+                    else:
+                        need = ["p" + op] if op[0] == "w" else []
+                    if not all(x in made for x in need):
+                        break
+                    todo[q].pop(0)
+                    made.add("p" + op if q == "p" else op)
+                    if q == "p" and op[0] == "w":
+                        spread(BANKS, k, 384, *["mn" + x[1] for x in need])
+                    elif q == "p":
+                        turn(EG, k, SETS, 24)
+                    elif op[0] == "g":
+                        vertices(EG, k, T.eno2)
+                    elif op[0] == "w":
+                        window(BANKS, k)
+                    else:
+                        b0, b1 = SETS[k]
+                        wait("v", "pm%d" % k, "g24", "srep")
+                        c = 384 * (b0 % 8) + 8 * (b0 // 8)
+                        inc(ve.tensor_tensor_scan(T.rep[:, c:c + 384 * (b1 - b0) - 8:16],
+                                                  T.m24[:, 0:24 * (b1 - b0)], T["t%d" % k][:, 0:24 * (b1 - b0)],
+                                                  1.0, A.max, A.min), "mn%d" % k)
+
+    places(False, T.pmo2, ("wv", "ws", "vp2"))
+    for k in range(len(LG)):
+        vertices(LG, k, T.eno2)
+        turn(LG, k, LSETS, 16)
+    c = 16 * LSETS[0][1]
+    wait("v", "pm0")
+    inc(ve.tensor_tensor_scan(T.red[:, 0:c], T.m16[:, 0:c], T.t0[:, 0:c], 1.0, A.max, A.min), "mn0")
+    for s in range(1, len(LSETS)):
+        wait("v", "pm%d" % s)
+        for b in range(*LSETS[s]):
+            c = 16 * (b - LSETS[s][0])
+            inc(ve.tensor_reduce(T.ys[:, b:b + 1], T["t%d" % s][:, c:c + 16], AxisListType.X, A.min), "vys")
+    wait("s", "mn0")
+    inc(se.activation(T.ys[:, 0:LSETS[0][1]], T.red[:, 15:16 * LSETS[0][1]:16], F.Copy), "sl")
+
+    wait("g", "vys", "sl")
+    m = topo.mask(core, order[0])
+    for c in order:
+        m &= topo.mask(core, c)
+    wide = len([e for e in topo.engines(core, order[0]) if m >> e & 1])
+    g.remote_dma_fused([RemoteDMATransfer(dst_ids=[did(c) for c in order], dma_engine_mask=m, remote_sem=T.sem.arrY,
+                                          srcs=[T.ys[:]], dsts=[T.land2[:, mine] for c in order])], local_sem=T.sem.loc)
+    n["loc"] += wide
+    n["arrY"] += wide * len(order)
+    wait("v", "vys", "sl")
     inc(ve.tensor_copy(T.land2[:, mine], T.ys[:]), "vown2")
-    wait(pe, "arrY", "vown2")
-    inc(pe.matmul(T.psT[:, 0:128], T.land2[:], T.ident[:], True, True), "pt")
-    wait(ve, "arrY", "vown2", "venc")
+    wait("p", "arrY", "vown2")
+    inc(pe.transpose(T.w0[:, 0:128], T.land2[:], T.ident[:]), "pt")
+    wait("v", "arrY", "vown2", "venc")
     inc(ve.tensor_tensor(T.flg[:], T.land2[:], T.enc[:], A.is_equal), "vflg")
-    wait(se, "pt")
-    inc(se.activation(T.lnv[:], T.psT[:, 0:128], F.Ln, scale=2.0 ** 32), "sln")
-    wait(ve, "sln", "sac")
+    wait("s", "pt")
+    inc(se.activation(T.lnv[:], T.w0[:, 0:128], F.Ln, scale=2.0 ** 32), "sln")
+    wait("v", "sln", "sac")
     inc(ve.tensor_scalar(T.yi[:], T.lnv[:], T.acol[:, 0:1], 1024.0, A.mult, A.add), "vyi")
-    wait(ve, "vyi")
+    wait("v", "vyi")
     inc(ve.tensor_copy(T.yf[:], T.yi[:]), "vyf")
-    wait(sy, "vyf")
+    wait("y", "vyf")
     inc(sy.dma_start(T.y[:], T.yf[:]), "dy", 16)
-    wait(pe, "vflg", "vones")
+    wait("p", "vflg", "vones")
     for b in range(16):
-        pc = pe.matmul(T.psR[0:8, 0:1], T.flg[:, b:128:16], T.ones[:, 0:1], b == 0, b == 15)
+        pc = pe.matmul(T.t3[0:8, 0:1], T.flg[:, b:128:16], T.ones[:, 0:1], b == 0, b == 15)
     inc(pc, "pc")
-    wait(se, "pc")
-    inc(se.activation(T.cf[0:8, 0:1], T.psR[0:8, 0:1], F.Copy), "scf")
-    wait(se, "scf")
+    wait("s", "pc")
+    inc(se.activation(T.cf[0:8, 0:1], T.t3[0:8, 0:1], F.Copy), "scf")
+    wait("s", "scf")
     inc(se.dma_start(T.cnt[:], T.cf[0:8, 0:1]), "dcnt", 16)
-    wait(sy, "dy")
-    wait(se, "dcnt")
-    wait(g, "loc")
+    wait("y", "dy")
+    wait("s", "dcnt")
+    wait("g", "loc")

@@ -4,48 +4,55 @@ from concourse.mybir import AluOpType as A, AxisListType, ActivationFunctionType
 
 BF, F32, I32, U16 = "bfloat16", "float32", "int32", "uint16"
 V = 2048
+RHO = 1 + 3 / 128
+SWIN = 6
 SCRATCH = {
-    "dtx": ("dram", [8, 128, 32], I32), "drx": ("dram", [8, 128, 32], I32),
-    "dst": ("dram", [8, 128, 16], BF), "drs": ("dram", [8, 128, 16], BF),
+    "ptx": ("dram", [8, 128, 32], I32), "prx": ("dram", [8, 128, 32], I32),
+    "ftx": ("dram", [2, 128, 64], BF), "frx": ("dram", [8, 128, 64], BF),
+    "pmi2": ("sbuf", [128, 128], I32), "eni2": ("sbuf", [128, 128], I32),
+    "sti": ("sbuf", [128, 128], I32), "stb": ("sbuf", [128, 128], BF),
+    "stt": ("sbuf", [128, 320], BF),
     "pmi": ("sbuf", [128, 128], I32), "eni": ("sbuf", [128, 128], I32),
     "pmo": ("sbuf", [128, 128], U16), "eno": ("sbuf", [128, 128], U16),
-    "pmi2": ("sbuf", [128, 128], I32), "eni2": ("sbuf", [128, 128], I32),
     "pmo2": ("sbuf", [128, 128], U16), "eno2": ("sbuf", [128, 128], U16),
     "stm": ("sbuf", [128, V], BF),
-    "win": ("sbuf", [128, V], BF), "plc": ("sbuf", [128, V], BF),
-    "cls": ("sbuf", [128, V], BF), "ver": ("sbuf", [128, V], BF),
-    "rep": ("sbuf", [128, 3072], BF), "red": ("sbuf", [128, 256], BF),
-    "xs": ("sbuf", [128, 128], BF), "land": ("sbuf", [128, 128], BF), "lr": ("sbuf", [128, 256], BF),
+    "win": ("sbuf", [128, V], BF), "plc": ("sbuf", [128, 3072], BF),
+    "cls": ("sbuf", [128, V], BF), "ver": ("sbuf", [128, V], BF), "red": ("sbuf", [128, 256], BF),
+    "x0": ("sbuf", [128, 512], BF), "x1": ("sbuf", [128, 512], BF),
+    "lr0": ("sbuf", [128, 128], BF), "lr1": ("sbuf", [128, 128], BF),
     "ys": ("sbuf", [128, 16], BF), "land2": ("sbuf", [128, 128], BF),
     "flg": ("sbuf", [128, 128], BF), "lnv": ("sbuf", [128, 128], F32),
     "yi": ("sbuf", [128, 128], I32), "yf": ("sbuf", [128, 128], F32), "cf": ("sbuf", [128, 4], F32),
-    "ones": ("sbuf", [128, 192], BF), "ident": ("sbuf", [128, 128], BF), "sel": ("sbuf", [128, 32], BF),
-    "m16": ("sbuf", [128, 192], BF), "m24": ("sbuf", [128, 192], BF), "ratio": ("sbuf", [128, 128], F32),
-    "enc": ("sbuf", [128, 128], BF), "c2": ("sbuf", [128, 4], F32), "lnc": ("sbuf", [128, 4], F32),
-    "acol": ("sbuf", [128, 4], F32), "hal": ("sbuf", [128, 8], BF),
-    "pi": ("sbuf", [128, 16], I32), "pa": ("sbuf", [128, 16], I32), "pl": ("sbuf", [128, 16], U16),
+    "ident": ("sbuf", [128, 128], BF), "sel": ("sbuf", [128, 32], BF),
+    "m16": ("sbuf", [128, 192], BF), "m24": ("sbuf", [128, 192], BF),
+    "ratio": ("sbuf", [128, 256], BF), "enc": ("sbuf", [128, 128], BF), "c2": ("sbuf", [128, 4], F32),
+    "lnc": ("sbuf", [128, 4], F32), "acol": ("sbuf", [128, 4], F32), "hal": ("sbuf", [128, 8], BF),
+    "pi": ("sbuf", [128, 8], I32), "pa": ("sbuf", [128, 8], I32), "pl": ("sbuf", [128, 8], U16),
     "t0": ("psum", [128, 512], F32), "t1": ("psum", [128, 512], F32), "t2": ("psum", [128, 512], F32),
     "t3": ("psum", [128, 512], F32),
     "w0": ("psum", [128, 1024], BF), "w1": ("psum", [128, 1024], BF), "w2": ("psum", [128, 1024], BF),
     "w3": ("psum", [128, 1024], BF),
 }
-SEMAPHORES = ("dpm den dtx down dlist dmask dy dcnt gd1 gd2 arrL arrS arrM arrY loc vones gident gsel gpi vstm vc2 sac "
-              "vrt vw0 sw1 sw2 sw3 vw4 sw4 vpm ven pe0 venc g16 g24 vrep srep vhal vp1 vp5 vp2 pg0 pg1 pg2 pg3 sc0 "
-              "sc1 sc2 sc3 eg0 eg1 eg2 eg3 eg4 eg5 eg6 eg7 pm0 pm1 pm2 pm3 mn0 mn1 mn2 mn3 pw0 pw1 pw2 pw3 wv ws vxs vown "
-              "vl sl vys vown2 pt sln vyi vyf vflg pc scf").split()
+SEMAPHORES = ("dpm dst den dtx dol doe dlist dle dfx df1 dy dcnt arrL arrF arrM0 arrM1 arrY loc "
+              "gones gident gsel gpi g16 vst vrt vw0 vw1 vpad pf0 penc sac senc vhal vp1 vp5 "
+              "win ps0 ps1 ps2 ps3 eg0 eg1 eg2 eg3 eg4 eg5 eg6 eg7 tx0 tx1 vx0 vx1 vl0 vl1 mx0 mx1 ta tb tc td mn0 mn1 mn2 mn3 g16b g24 srep "
+              "pw0 pw1 pw2 pw3 vys pt sln0 sln1 vyi0 vyi1 vyf vflg pc scf").split()
 
-PCUT = [("v", 768), ("s", 1536), ("s", 2048)]
-PV = ["g0", "c1", "c2"]
-EG = [("s", 0, 4), ("v", 8, 12), ("s", 4, 7), ("s", 7, 8), ("v", 12, 16)]
-SETS = [(0, 4), (8, 12), (4, 8), (12, 16)]
-BANKS = [("s", 0, 1), ("v", 1, 4), ("v", 4, 6), ("s", 6, 8)]
-EV = ["g1", "g4", "m1", "m0", "m3", "m2", "w1", "w2"]
-ES = ["g0", "g2", "g3", "w0", "w3"]
-EP = ["g0", "g1", "g2", "g4", "g3", "w0", "w1", "w3", "w2"]
-XBANKS = [("s", 0, 1), ("v", 1, 3), ("s", 3, 5), ("v", 5, 8)]
-FG = [("v", 0, 6), ("s", 8, 14), ("v", 6, 8), ("s", 14, 16)]
-LG = [("v", 0, 6), ("s", 6, 12), ("v", 12, 14), ("s", 14, 16)]
-LSETS = [(0, 12), (12, 14), (14, 16)]
+PCUT = [("v", 736), ("s", 1408), ("s", 1984), ("v", 2048)]
+PV = ["g0", "g3", "c1", "c3"]
+PCUT1 = [("v", 256), ("s", 512), ("v", 896), ("s", 1408), ("s", 1920), ("v", 2048)]
+PV1 = ["g0", "flags", "g2", "c1", "g5", "c3", "en", "c5"]
+EG = [("v", 0, 4), ("v", 4, 5), ("v", 5, 8), ("s", 8, 13), ("s", 13, 16)]
+SETS = [(0, 4), (4, 8), (8, 13), (13, 16)]
+BANKS = [("s", 0, 2), ("v", 2, 4), ("s", 4, 5), ("v", 5, 8)]
+EV = ["g0", "g2", "g1", "m0", "m2", "m3", "m1", "w1", "w3"]
+ES = ["g3", "g4", "w0", "w2"]
+EP = ["g0", "g3", "g2", "g4", "g1", "w0", "w1", "w3", "w2"]
+XBANKS = [("s", 0, 3), ("v", 3, 4), ("v", 4, 7), ("s", 7, 8)]
+FG = [("v", 0, 2), ("s", 8, 11), ("v", 2, 4), ("s", 11, 12), ("v", 4, 6), ("s", 12, 15), ("v", 6, 8), ("s", 15, 16)]
+FSHIP = 6
+LG = [("v", 0, 4), ("s", 4, 9), ("v", 9, 12), ("s", 12, 15), ("v", 15, 16)]
+LSETS = [(0, 12), (12, 16)]
 
 
 def rank_program(g, core, T, topo):
@@ -67,29 +74,58 @@ def rank_program(g, core, T, topo):
                 Q[q].wait_ge(T.sem[s], n[s])
                 seen[(q, s)] = n[s]
 
+    def ring(src):
+        far = [c for c in T.cores if topo.die(c) != topo.die(src)]
+        near = [c for c in T.cores if topo.die(c) == topo.die(src) and c != src]
+        turn = T.rank_of(src) % len(far)
+        far = far[turn:] + far[:turn]
+        out = []
+        while far or near:
+            if far:
+                out.append(far.pop(0))
+            if near:
+                out.append(near.pop(0))
+        return out
     others = [c for c in T.cores if c != core]
-    far = [c for c in others if topo.die(c) != topo.die(core)]
-    near = [c for c in others if topo.die(c) == topo.die(core)]
-    order = []
-    while far or near:
-        if far:
-            order.append(far.pop(0))
-        if near:
-            order.append(near.pop(0))
+    order = ring(core)
+
+    def first_of_die(c):
+        return min(T.rank_of(d) for d in T.cores if topo.die(d) == topo.die(c))
 
     def did(c):
         rid, pid, _s = topo.addr(c)
         return DstId(rid=rid, pnc=pid)
 
-    def send(src_of, dst, arr):
+    def to_all(ap, arr):
+        m = topo.mask(core, order[0])
+        for c in order:
+            m &= topo.mask(core, c)
+        g.remote_dma_fused([RemoteDMATransfer(dst_ids=[did(c) for c in order], dma_engine_mask=m, remote_sem=T.sem[arr],
+                                              srcs=[ap], dsts=[ap for c in order])], local_sem=T.sem.loc)
+        n["loc"] += bin(m).count("1")
+        n[arr] += bin(m).count("1") * len(order)
+
+    def each(tx, rx, arr):
         trs = []
         for k, c in enumerate(order):
             e = topo.engines(core, c)
-            m = (1 << e[k]) | (1 << e[k + len(e) // 2])
+            half = len(e) // 2
+            m = sum((1 << e[i]) | (1 << e[i + half]) for i in ([k] if k else [k] + list(range(len(order), half))))
             trs.append(RemoteDMATransfer(dst_ids=[did(c)], dma_engine_mask=m, remote_sem=T.sem[arr],
-                                         src=src_of(T.rank_of(c)), dst=dst))
-            n["loc"] += 2
-            n[arr] += 2
+                                         src=tx[T.rank_of(c)], dst=rx[me]))
+            n["loc"] += bin(m).count("1")
+        g.remote_dma_fused(trs, local_sem=T.sem.loc)
+        n[arr] += sum(4 if ring(c)[0] == core else 2 for c in others)
+
+    def by_die(arr, src_of, dst_of):
+        trs = []
+        for k, across in enumerate((True, False)):
+            to = [c for c in order if (topo.die(c) != topo.die(core)) == across]
+            e = topo.engines(core, to[0])[k::2]
+            trs.append(RemoteDMATransfer(dst_ids=[did(c) for c in to], dma_engine_mask=sum(1 << i for i in e),
+                                         remote_sem=T.sem[arr], srcs=[src_of(to[0])], dsts=[dst_of(c) for c in to]))
+            n["loc"] += len(e)
+            n[arr] += len(e) * len(to)
         g.remote_dma_fused(trs, local_sem=T.sem.loc)
 
     def gather(q, out, win, off, name):
@@ -98,170 +134,224 @@ def rank_program(g, core, T, topo):
         else:
             inc(se.activation(out, win.indirect(off), F.Copy), name)
 
-    inc(sy.dma_start(T.pmi[:], T.pm[:]), "dpm", 16)
-    inc(ve.memset(T.ratio[:], 2.0 ** (1.0 / 32)), "vrt")
-    wait("v", "vrt")
-    inc(ve.tensor_tensor_scan(T.win[:, 0:128], T.ratio[:], T.ratio[:], 2.0 ** (-64 - 1.0 / 32), A.mult, A.min), "vw0")
-    inc(ve.memset(T.stm[:], 0.0), "vstm")
-    inc(ve.memset(T.ones[:], 1.0), "vones")
-    inc(ve.memset(T.c2[:, 0:2], math.exp(16.0 / math.log(2.0))), "vc2")
-    for k, (a, b) in enumerate((("vw0", "sw1"), ("sw1", "sw2"), ("sw2", "sw3"))):
-        w = 128 << k
-        wait("s", a)
-        inc(se.activation(T.win[:, w:2 * w], T.win[:, 0:w], F.Copy, scale=2.0 ** (w // 32)), b)
-    wait("s", "sw3")
-    inc(se.activation(T.win[:, 1728:2048], T.win[:, 704:1024], F.Copy, scale=2.0 ** 32), "sw4")
-    wait("v", "dpm")
-    inc(ve.tensor_copy(T.pmo[:], T.pmi[:]), "vpm")
-    wait("v", "sw3")
-    inc(ve.tensor_scalar(T.win[:, 1024:1728], T.win[:, 0:704], 2.0 ** 32, None, A.mult), "vw4")
-
-    wait("g", "vstm")
-    inc(g.dma_start(T.stm[0:128:16, :], T.st[:]), "gd1", 16)
-    inc(g.dma_start(T.dst[:], T.st[:]), "gd2", 16)
-    wait("g", "vones")
-    inc(g.affine_select(T.sel[:], T.ones[:, 0:32], [[0, 2], [-8, 16]], A.is_equal, 0.0, 0, 1), "gsel")
-    inc(g.affine_select(T.ident[:], T.ones[:, 0:128], [[-1, 128]], A.is_equal, 0.0, 0, 1), "gident")
-    inc(g.iota(T.pi[:], [[1, 16]], 0, 16), "gpi")
-    sel8 = T.sel[:, 0:16:2]
-
-    wait("y", "dpm")
-    inc(sy.dma_start(T.eni[:], T.en[:]), "den", 16)
-    inc(sy.dma_start(T.dtx[:, 0:64, :], T.pm[:]), "dtx", 16)
-    inc(sy.dma_start(T.dtx[:, 64:128, :], T.en[:]), "dtx", 16)
-    own = slice(16 * me, 16 * me + 16)
-    inc(sy.dma_start(T.drx[me, 0:64, :], T.pm[own, :]), "down", 16)
-    inc(sy.dma_start(T.drx[me, 64:128, :], T.en[own, :]), "down", 16)
-
-    wait("g", "dtx")
-    send(lambda r: T.dtx[r], T.drx[me], "arrL")
-    wait("g", "gd2")
-    send(lambda r: T.dst[r], T.drs[me], "arrS")
-    wait("y", "gd2")
-    inc(sy.dma_start(T.drs[me], T.dst[me]), "down", 16)
-    wait("y", "down", "arrL")
-    inc(sy.dma_start(T.pmi2[:], T.drx[:, 0:64, :]), "dlist", 16)
-    inc(sy.dma_start(T.eni2[:], T.drx[:, 64:128, :]), "dlist", 16)
-
-    wait("p", "vw4", "sw4", "gsel")
-    for b in range(16):
-        inc(pe.matmul(T.t1[:, b:128:16], T.win[:, 128 * b:128 * b + 128], sel8, True, True), "pe0")
-
-    def places(first, pmo, ready):
-        wait("v", *ready)
-        wait("s", *ready)
-        lo = [0] + [e for _q, e in PCUT]
+    def places(cut, vector_order, plc, pmo, flags, ready, scalar_gap=None):
+        for q in "vs":
+            wait(q, *ready)
+        lo = [0] + [e for _q, e in cut]
+        ends = [int(op[1]) for op in vector_order if op[0] == "c"]
 
         def piece(k):
             a, b = lo[k], lo[k + 1]
-            gather(PCUT[k][0], T.plc[:, a:b], T.win[:], pmo[:, a // 16:b // 16], "pg%d" % k)
-        for k in range(len(PCUT)):
-            if PCUT[k][0] == "s":
+            gather(cut[k][0], plc[:, a:b], T.win[:], pmo[:, a // 16:b // 16], "ps%d" % len([e for e in ends if e < k]))
+        for k in range(len(cut)):
+            if cut[k][0] == "s":
                 piece(k)
+        if scalar_gap:
+            scalar_gap()
         done, scans = 0, 0
-        for op in PV:
+        for op in vector_order:
+            if op in ("flags", "en"):
+                flags_turned() if op == "flags" else en_offsets()
+                continue
             k = int(op[1])
             if op[0] == "g":
                 piece(k)
                 continue
-            if first and not scans:
-                wait("v", "den")
-                inc(ve.tensor_copy(T.eno[:], T.eni[:]), "ven")
-            wait("v", "gd1" if first else "dmask", *["pg%d" % j for j in range(done, k + 1)])
             a, b = lo[done], lo[k + 1]
-            if scans:
-                wait("v", "sc%d" % (scans - 1))
-            inc(ve.tensor_tensor_scan(T.cls[:, a:b], T.stm[:, a:b], T.plc[:, a:b],
-                                      T.cls[:, a - 1:a] if scans else 1.0, A.max, A.min), "sc%d" % scans)
+            marks = flags(a, b)
+            wait("v", "ps%d" % scans)
+            inc(ve.tensor_tensor_scan(T.cls[:, a:b], marks, plc[:, a:b],
+                                      T.cls[:, a - 1:a] if scans else 1.0, A.max, A.min), "ps%d" % (scans + 1))
             done, scans = k + 1, scans + 1
         for q in "vs":
-            wait(q, "sc%d" % (scans - 1), "ven")
-        return "sc%d" % (scans - 1)
+            wait(q, "ps%d" % scans)
+        return "ps%d" % scans
 
-    def vertices(pieces, k, eno):
-        q, b0, b1 = pieces[k]
-        gather(q, T.ver[:, 128 * b0:128 * b1], T.cls[:], eno[:, 8 * b0:8 * b1], "eg%d" % k)
+    own = slice(16 * me, 16 * me + 16)
+    inc(sy.dma_start(T.pmi[:], T.pm[:]), "dpm", 16)
+    inc(sy.dma_start(T.sti[:], T.st[:]), "dst", 16)
+    inc(sy.dma_start(T.ptx[:, 0:64, :], T.pm[:]), "dtx", 16)
+    inc(sy.dma_start(T.ptx[:, 64:128, :], T.en[:]), "dtx", 16)
+    inc(sy.dma_start(T.eni[:], T.en[:]), "den", 16)
+    inc(ve.memset(T.ratio[:], RHO), "vrt")
 
-    def set_of(sets, b):
-        return [s for s, (b0, b1) in enumerate(sets) if b0 <= b < b1][0]
+    def ones(k):
+        return T.stt[:, 128:128 + k]
+    inc(g.iota(ones(192), [[0, 192]], 1, 0, allow_small_or_imprecise_dtypes=True), "gones")
+    wait("g", "gones")
+    inc(g.affine_select(T.ident[:], ones(128), [[-1, 128]], A.is_equal, 0.0, 0, 1), "gident")
+    inc(g.affine_select(T.sel[:], ones(32), [[0, 2], [-8, 16]], A.is_equal, 0.0, 0, 1), "gsel")
+    sel8 = T.sel[:, 0:16:2]
+    wait("v", "vrt")
+    inc(ve.tensor_tensor_scan(T.win[:, 0:256], T.ratio[:], T.ratio[:], RHO ** (-V - 1), A.mult, A.min), "vw0")
+    wait("v", "vw0")
+    wait("s", "vw0")
+    for k in range(1, 8):
+        dst, f = T.win[:, 256 * k:256 * k + 256], RHO ** (256 * k)
+        if k < SWIN:
+            inc(ve.tensor_scalar(dst, T.win[:, 0:256], f, None, A.mult), "win")
+        else:
+            inc(se.activation(dst, T.win[:, 0:256], F.Copy, scale=f), "win")
+    wait("v", "dpm")
+    inc(ve.tensor_copy(T.pmo[:], T.pmi[:]), "win")
+    wait("v", "dst")
+    inc(ve.tensor_copy(T.stb[:], T.sti[:]), "vst")
+    wait("p", "vst", "gident")
+    inc(pe.transpose(T.w2[:, 0:128], T.stb[:], T.ident[:]), "pf0")
+    fend = [PCUT1[int(op[1])][1] for op in PV1 if op[0] == "c"]
 
-    def spread(banks, k, step, *ready):
-        _q, b0, b1 = banks[k]
-        wait("p", "gident", *ready)
-        for b in range(b0, b1):
-            inc(pe.transpose(T["w%d" % k][:, 128 * (b - b0):128 * (b - b0 + 1)],
-                             T.rep[:, step * b + 256:step * b + 384], T.ident[:]), "pw%d" % k)
+    def flag_bank(a):
+        s = len([e for e in fend if e <= a])
+        return s, T["w%d" % (0, 1, 3)[s]], ([0] + fend)[s]
 
-    def window(banks, k):
-        q, b0, b1 = banks[k]
-        src = T["w%d" % k][:, 0:128 * (b1 - b0)]
-        wait(q, "pw%d" % k, "vhal")
-        for h in (0, 1):
-            dst, blank = T.win[:, 1024 * h + 128 * b0:1024 * h + 128 * b1], T.hal[:, 1 - h:2 - h]
-            if q == "v":
-                inc(ve.tensor_scalar(dst, src, blank, None, A.max), "wv")
-            else:
-                inc(se.activation(dst, src, F.Identity, bias=blank), "ws")
+    def flags_turned():
+        wait("v", "pf0")
+        inc(ve.tensor_copy(T.stt[:, 0:128], T.w2[:, 0:128]), "vpad")
+        wait("p", "vpad")
+        for k in range(16):
+            s, bank, lo = flag_bank(128 * k)
+            inc(pe.transpose(bank[:, 128 * k - lo:128 * k - lo + 128], T.stt[:, k:k + 128], T.ident[:]), "ps%d" % s)
+        for b in range(16):
+            inc(pe.matmul(T.t2[:, b:128:16], T.win[:, 128 * b:128 * b + 128], sel8, True, True), "penc")
+    wait("g", "dtx")
+    each(T.ptx, T.prx, "arrL")
+    inc(g.iota(T.pi[:], [[1, 8]], 8 * (me - first_of_die(core)), 32), "gpi")
+    inc(g.affine_select(T.m16[:, 0:64], ones(64), [[0, 4], [1, 16]], A.is_equal, 0.0, 0, 0), "g16")
+    mine = slice(32 * (me - first_of_die(core)), 32 * (me - first_of_die(core)) + 32)
+    wait("y", "dtx")
+    inc(sy.dma_start(T.prx[me], T.ptx[me]), "dol", 16)
+    wait("p", "gsel", "win")
 
-    scanned = places(True, T.pmo, ("vw4", "sw4", "vpm"))
-    wait("y", scanned, "arrS", "down")
+    def idle_columns(*pairs):
+        wait("s", "gones")
+        for b in pairs:
+            inc(se.activation(T.plc[:, 384 * b + 256:384 * b + 384], ones(128), F.Copy), "srep")
+
+    def en_offsets():
+        wait("v", "den")
+        inc(ve.tensor_copy(T.eno[:], T.eni[:]), "ps3")
+
+    def bank_flags(a, b):
+        return flag_bank(a)[1][:, 0:b - a]
+
+    scanned = places(PCUT1, PV1, T.stm, T.pmo, bank_flags, ("win",), lambda: idle_columns(5, 6))
+    wait("y", "vst")
+    inc(sy.dma_start(T.ftx[:], T.stb[:]), "dfx", 16)
+    inc(sy.dma_start(T.frx[me, mine, :], T.stb[own, :]), "doe", 16)
+    wait("y", "dol", "arrL")
+    inc(sy.dma_start(T.pmi2[:], T.prx[:, 0:64, :]), "dlist", 16)
+    inc(sy.dma_start(T.eni2[:], T.prx[:, 64:128, :]), "dle", 16)
+
+    def vertices(piece, name, eno):
+        q, b0, b1 = piece
+        gather(q, T.ver[:, 128 * b0:128 * b1], T.cls[:], eno[:, 8 * b0:8 * b1], name)
+
+    def slab(s, *pieces):
+        for name, b0, b1 in pieces:
+            wait("p", name, "gsel")
+            for b in range(b0, b1):
+                j = b % 4 + 4 * (b // 8)
+                inc(pe.matmul(T["t%d" % s][:, j:64:8], T.ver[:, 128 * b:128 * b + 128], sel8, True, True), "tx%d" % s)
+
+    def ship(s):
+        x = T["x%d" % s]
+        wait("v", "tx%d" % s)
+        base = 0 if first_of_die(core) else 256
+        inc(ve.tensor_copy(x[:, base:base + 64], T["t%d" % s][:, 0:64]), "vx%d" % s)
+        wait("g", "vx%d" % s)
+
+        def cols(a):
+            return x[:, a:a + 32]
+        by_die("arrM%d" % s, lambda c: cols(base + 8 * first_of_die(c)),
+               lambda c: cols((32 if first_of_die(c) else 0) + 32 * ((me - T.rank_of(c)) % 8)))
+
+    for k, p in enumerate(FG):
+        if k == FSHIP:
+            ship(0)
+        vertices(p, "eg%d" % k, T.eno)
+        slab(p[1] % 8 // 4, ("eg%d" % k, p[1], p[2]))
+    ship(1)
+    wait("g", "dfx")
+    by_die("arrF", lambda c: T.ftx[min(first_of_die(c), 1)], lambda c: T.frx[me])
+    wait("y", "arrF", scanned, "doe")
     for h in (0, 8):
-        inc(sy.dma_start(T.stm[h:128:16, :], T.drs[0:8]), "dmask", 16)
-    for k in range(len(FG)):
-        vertices(FG, k, T.eno)
-    for k, (_q, b0, b1) in enumerate(FG):
-        wait("p", "eg%d" % k)
-        for b in range(b0, b1):
-            inc(pe.matmul(T.t0[:, b:128:16], T.ver[:, 128 * b:128 * b + 128], sel8, True, True), "pm0")
-    wait("v", "pm0")
-    inc(ve.tensor_copy(T.xs[:], T.t0[:, 0:128]), "vxs")
-    wait("g", "vxs")
-    mine = slice(16 * me, 16 * me + 16)
-    send(lambda r: T.xs[:, 16 * r:16 * r + 16], T.land[:, mine], "arrM")
-    wait("v", "vxs")
-    inc(ve.tensor_copy(T.land[:, mine], T.xs[:, mine]), "vown")
-    wait("s", "vc2")
-    inc(se.activation(T.lnc[:, 0:2], T.c2[:, 0:2], F.Ln, accum_out=T.acol[:, 0:1]), "sac")
-    inc(g.affine_select(T.m16[:], T.ones[:], [[0, 12], [1, 16]], A.is_equal, 0.0, 0, 0), "g16")
-    inc(g.affine_select(T.m24[:], T.ones[:], [[0, 8], [1, 24]], A.is_equal, 0.0, 0, 0), "g24")
-    inc(ve.memset(T.rep[:, 256:2304], 1.0), "vrep")
-    wait("s", "vones")
-    for b in (6, 7):
-        inc(se.activation(T.rep[:, 384 * b + 256:384 * b + 384], T.ones[:, 0:128], F.Copy), "srep")
-    wait("v", "gpi", "gsel")
-    inc(ve.tensor_scalar(T.pa[:], T.pi[:], 127, None, A.bitwise_and), "vp1")
+        inc(sy.dma_start(T.stm[h:128:16, :], T.frx[:, mine, :]), "df1", 16)
+    inc(g.affine_select(T.m24[:], ones(192), [[0, 8], [1, 24]], A.is_equal, 0.0, 0, 0), "g24")
+    inc(g.affine_select(T.m16[:, 64:192], ones(128), [[0, 8], [1, 16]], A.is_equal, 0.0, 0, 0), "g16b")
+    wait("v", "gpi", "penc")
+    inc(ve.tensor_scalar(T.pa[:], T.pi[:], 255, None, A.bitwise_and), "vp1")
     for h in (0, 1):
         inc(ve.tensor_reduce(T.hal[:, h:h + 1], T.sel[:, h:16:2], AxisListType.X, A.max), "vhal")
     wait("v", "vp1")
     inc(ve.tensor_copy(T.pl[:], T.pa[:]), "vp5")
     wait("v", "dlist")
-    inc(ve.tensor_copy(T.pmo2[:], T.pmi2[:]), "vp2")
-    inc(ve.tensor_copy(T.eno2[:], T.eni2[:]), "vp2")
-    wait("s", "pe0")
-    inc(se.activation(T.enc[:], T.t1[:, 0:128], F.Copy), "venc")
-    for h, q in enumerate("vs"):
-        wait(q, "arrM", "vown", "vp5")
-        gather(q, T.lr[:, 128 * h:128 * h + 128], T.land[:], T.pl[:, 8 * h:8 * h + 8], q + "l")
-    for h, q in enumerate("vs"):
-        wait("v", q + "l", "g16", "vrep")
-        inc(ve.tensor_tensor_scan(T.rep[:, 128 + 8 * h:2176:16], T.m16[:, 0:128], T.lr[:, 128 * h:128 * h + 128],
-                                  1.0, A.max, A.min), "mn%d" % h)
-    for k in range(len(XBANKS)):
-        spread(XBANKS, k, 256, "mn0", "mn1")
+    inc(ve.tensor_copy(T.pmo2[:], T.pmi2[:]), "win")
+    wait("v", "g16", "vp5", "vhal")
+    wait("p", "gident")
+    inc(se.activation(T.lnc[:, 0:2], ones(2), F.Ln, scale=math.exp(0.5 / math.log(RHO)),
+                      accum_out=T.acol[:, 0:1]), "sac")
+    wait("s", "vhal")
+
+    def spread(banks, k, rep, first, step, *ready):
+        _q, b0, b1 = banks[k]
+        wait("p", *ready)
+        for b in range(b0, b1):
+            c = first + step * b
+            inc(pe.transpose(T["w%d" % k][:, 128 * (b - b0):128 * (b - b0 + 1)], rep[:, c:c + 128], T.ident[:]),
+                "pw%d" % k)
+
+    def window(banks, k):
+        q, b0, b1 = banks[k]
+        src = T["w%d" % k][:, 0:128 * (b1 - b0)]
+        wait(q, "pw%d" % k)
+        for h in (0, 1):
+            dst, blank = T.win[:, 1024 * h + 128 * b0:1024 * h + 128 * b1], T.hal[:, 1 - h:2 - h]
+            if q == "v":
+                inc(ve.tensor_scalar(dst, src, blank, None, A.max), "win")
+            else:
+                inc(se.activation(dst, src, F.Identity, bias=blank), "win")
+
+    for s in (0, 1):
+        lr = T["lr%d" % s]
+        wait("v", "vx0", "vx1", "arrM%d" % s)
+        for h in (0, 1):
+            gather("v", lr[:, 64 * h:64 * h + 64], T["x%d" % s][:, 32:288], T.pl[:, 4 * h:4 * h + 4], "vl%d" % h)
+        for h in (0, 1):
+            c = 1024 * s + 8 * h
+            wait("v", "vl%d" % h)
+            inc(ve.tensor_tensor_scan(T.cls[:, c:c + 1016:16], T.m16[:, 0:64], lr[:, 64 * h:64 * h + 64],
+                                      1.0, A.max, A.min), "mx%d" % s)
+        for k in (2 * s, 2 * s + 1):
+            spread(XBANKS, k, T.cls, 128, 256, "mx%d" % s)
+        if not s:
+            wait("v", "dle")
+            inc(ve.tensor_copy(T.eno2[:], T.eni2[:]), "win")
     for k in range(len(XBANKS)):
         window(XBANKS, k)
 
-    def turn(pieces, k, sets, wide):
+    def set_of(sets, b):
+        return [s for s, (b0, b1) in enumerate(sets) if b0 <= b < b1][0]
+
+    def turn(pieces, k, sets, wide, names):
         _q, b0, b1 = pieces[k]
         s = set_of(sets, b0)
-        wait("p", "eg%d" % k, "venc")
+        wait("p", "senc", "eg%d" % k)
         for b in range(b0, b1):
             c = wide * (b - sets[s][0])
             inc(pe.matmul(T["t%d" % s][:, c:c + wide], T.ver[:, 128 * b:128 * b + 128], T.sel[:, 0:wide], True, True),
-                "pm%d" % s)
+                names[s])
 
-    for _hop in (2, 3):
-        places(False, T.pmo2, ("wv", "ws", "vp2"))
+    def row_flags(a, b):
+        wait("v", "df1")
+        return T.stm[:, a:b]
+
+    def codes_and_columns():
+        wait("s", "penc")
+        inc(se.activation(T.enc[:], T.t2[:, 0:128], F.Copy), "senc")
+        idle_columns(7)
+
+    for hop in (2, 3):
+        places(PCUT, PV, T.plc, T.pmo2, row_flags, ("win",), codes_and_columns if hop == 2 else None)
         todo = {"v": list(EV), "s": list(ES), "p": list(EP)}
         made = set()
         while todo["v"] or todo["s"] or todo["p"]:
@@ -270,7 +360,7 @@ def rank_program(g, core, T, topo):
                     op = todo[q][0]
                     k = int(op[1])
                     if q == "p" and op[0] == "w":
-                        need = ["m%d" % set_of(SETS, BANKS[k][1] + h) for h in (0, 8)]
+                        need = sorted(set("m%d" % set_of(SETS, b + h) for b in range(*BANKS[k][1:]) for h in (0, 8)))
                     elif q == "p":
                         need = [op]
                     elif op[0] == "m":
@@ -282,62 +372,54 @@ def rank_program(g, core, T, topo):
                     todo[q].pop(0)
                     made.add("p" + op if q == "p" else op)
                     if q == "p" and op[0] == "w":
-                        spread(BANKS, k, 384, *["mn" + x[1] for x in need])
+                        spread(BANKS, k, T.plc, 256, 384, "srep", *["mn" + x[1] for x in need])
                     elif q == "p":
-                        turn(EG, k, SETS, 24)
+                        turn(EG, k, SETS, 24, ("ta", "tb", "tc", "td"))
                     elif op[0] == "g":
-                        vertices(EG, k, T.eno2)
+                        vertices(EG[k], "eg%d" % k, T.eno2)
                     elif op[0] == "w":
                         window(BANKS, k)
                     else:
                         b0, b1 = SETS[k]
-                        wait("v", "pm%d" % k, "g24", "srep")
+                        wait("v", "g24", "srep", ("ta", "tb", "tc", "td")[k])
                         c = 384 * (b0 % 8) + 8 * (b0 // 8)
-                        inc(ve.tensor_tensor_scan(T.rep[:, c:c + 384 * (b1 - b0) - 8:16],
+                        inc(ve.tensor_tensor_scan(T.plc[:, c:c + 384 * (b1 - b0) - 8:16],
                                                   T.m24[:, 0:24 * (b1 - b0)], T["t%d" % k][:, 0:24 * (b1 - b0)],
                                                   1.0, A.max, A.min), "mn%d" % k)
 
-    places(False, T.pmo2, ("wv", "ws", "vp2"))
+    places(PCUT, PV, T.plc, T.pmo2, row_flags, ("win",))
     for k in range(len(LG)):
-        vertices(LG, k, T.eno2)
-        turn(LG, k, LSETS, 16)
-    c = 16 * LSETS[0][1]
-    wait("v", "pm0")
-    inc(ve.tensor_tensor_scan(T.red[:, 0:c], T.m16[:, 0:c], T.t0[:, 0:c], 1.0, A.max, A.min), "mn0")
-    for s in range(1, len(LSETS)):
-        wait("v", "pm%d" % s)
-        for b in range(*LSETS[s]):
-            c = 16 * (b - LSETS[s][0])
-            inc(ve.tensor_reduce(T.ys[:, b:b + 1], T["t%d" % s][:, c:c + 16], AxisListType.X, A.min), "vys")
-    wait("s", "mn0")
-    inc(se.activation(T.ys[:, 0:LSETS[0][1]], T.red[:, 15:16 * LSETS[0][1]:16], F.Copy), "sl")
+        vertices(LG[k], "eg%d" % k, T.eno2)
+        turn(LG, k, LSETS, 16, ("ta", "tb"))
+    for s, (b0, b1) in enumerate(LSETS):
+        c = 16 * (b1 - b0)
+        wait("v", "g16b", ("ta", "tb")[s])
+        inc(ve.tensor_tensor_scan(T.red[:, 16 * b0:16 * b1], T.m16[:, 0:c], T["t%d" % s][:, 0:c], 1.0, A.max, A.min),
+            "mn0")
+    wait("v", "mn0")
+    inc(ve.tensor_copy(T.land2[:, own], T.red[:, 15:256:16]), "vys")
 
-    wait("g", "vys", "sl")
-    m = topo.mask(core, order[0])
-    for c in order:
-        m &= topo.mask(core, c)
-    wide = len([e for e in topo.engines(core, order[0]) if m >> e & 1])
-    g.remote_dma_fused([RemoteDMATransfer(dst_ids=[did(c) for c in order], dma_engine_mask=m, remote_sem=T.sem.arrY,
-                                          srcs=[T.ys[:]], dsts=[T.land2[:, mine] for c in order])], local_sem=T.sem.loc)
-    n["loc"] += wide
-    n["arrY"] += wide * len(order)
-    wait("v", "vys", "sl")
-    inc(ve.tensor_copy(T.land2[:, mine], T.ys[:]), "vown2")
-    wait("p", "arrY", "vown2")
+    wait("g", "vys")
+    to_all(T.land2[:, own], "arrY")
+    wait("p", "vys", "arrY")
     inc(pe.transpose(T.w0[:, 0:128], T.land2[:], T.ident[:]), "pt")
-    wait("v", "arrY", "vown2", "venc")
+    wait("v", "senc", "sac", "vys", "arrY")
     inc(ve.tensor_tensor(T.flg[:], T.land2[:], T.enc[:], A.is_equal), "vflg")
     wait("s", "pt")
-    inc(se.activation(T.lnv[:], T.w0[:, 0:128], F.Ln, scale=2.0 ** 32), "sln")
-    wait("v", "sln", "sac")
-    inc(ve.tensor_scalar(T.yi[:], T.lnv[:], T.acol[:, 0:1], 1024.0, A.mult, A.add), "vyi")
-    wait("v", "vyi")
-    inc(ve.tensor_copy(T.yf[:], T.yi[:]), "vyf")
+    halves = [(h, slice(64 * h, 64 * h + 64)) for h in (0, 1)]
+    for h, c in halves:
+        inc(se.activation(T.lnv[:, c], T.w0[:, c], F.Ln, scale=RHO ** 1024), "sln%d" % h)
+    for h, c in halves:
+        wait("v", "sln%d" % h, "sac")
+        inc(ve.tensor_scalar(T.yi[:, c], T.lnv[:, c], T.acol[:, 0:1], 1024.0, A.mult, A.add), "vyi%d" % h)
+    for h, c in halves:
+        wait("v", "vyi%d" % h)
+        inc(ve.tensor_copy(T.yf[:, c], T.yi[:, c]), "vyf")
     wait("y", "vyf")
     inc(sy.dma_start(T.y[:], T.yf[:]), "dy", 16)
-    wait("p", "vflg", "vones")
+    wait("p", "vflg")
     for b in range(16):
-        pc = pe.matmul(T.t3[0:8, 0:1], T.flg[:, b:128:16], T.ones[:, 0:1], b == 0, b == 15)
+        pc = pe.matmul(T.t3[0:8, 0:1], T.flg[:, b:128:16], ones(1), b == 0, b == 15)
     inc(pc, "pc")
     wait("s", "pc")
     inc(se.activation(T.cf[0:8, 0:1], T.t3[0:8, 0:1], F.Copy), "scf")

import math
from concourse.bass import DstId, RemoteDMATransfer
from concourse.mybir import AluOpType as A, AxisListType, ActivationFunctionType as F

BF, F32, I32, U16 = "bfloat16", "float32", "int32", "uint16"
V = 2048
RHO = 1 + 3 / 128
SWIN = 6
SCRATCH = {
    "ptx": ("dram", [8, 128, 32], I32), "prx": ("dram", [8, 128, 32], I32),
    "ftx": ("dram", [2, 128, 64], BF), "frx": ("dram", [8, 128, 64], BF),
    "pmi2": ("sbuf", [128, 128], I32), "eni2": ("sbuf", [128, 128], I32),
    "sti": ("sbuf", [128, 128], I32), "stb": ("sbuf", [128, 128], BF),
    "stt": ("sbuf", [128, 320], BF),
    "pmi": ("sbuf", [128, 128], I32), "eni": ("sbuf", [128, 128], I32),
    "pmo": ("sbuf", [128, 128], U16), "eno": ("sbuf", [128, 128], U16),
    "pmo2": ("sbuf", [128, 128], U16), "eno2": ("sbuf", [128, 128], U16),
    "stm": ("sbuf", [128, V], BF),
    "win": ("sbuf", [128, V], BF), "plc": ("sbuf", [128, 3072], BF),
    "cls": ("sbuf", [128, V], BF), "ver": ("sbuf", [128, V], BF), "red": ("sbuf", [128, 256], BF),
    "x0": ("sbuf", [128, 512], BF), "x1": ("sbuf", [128, 512], BF),
    "lr0": ("sbuf", [128, 128], BF), "lr1": ("sbuf", [128, 128], BF),
    "ys": ("sbuf", [128, 16], BF), "land2": ("sbuf", [128, 128], BF),
    "flg": ("sbuf", [128, 128], BF), "lnv": ("sbuf", [128, 128], F32),
    "yi": ("sbuf", [128, 128], I32), "yf": ("sbuf", [128, 128], F32), "cf": ("sbuf", [128, 4], F32),
    "ident": ("sbuf", [128, 128], BF), "sel": ("sbuf", [128, 32], BF),
    "m16": ("sbuf", [128, 192], BF), "m24": ("sbuf", [128, 192], BF),
    "ratio": ("sbuf", [128, 256], BF), "enc": ("sbuf", [128, 128], BF), "c2": ("sbuf", [128, 4], F32),
    "lnc": ("sbuf", [128, 4], F32), "acol": ("sbuf", [128, 4], F32), "hal": ("sbuf", [128, 8], BF),
    "pi": ("sbuf", [128, 8], I32), "pa": ("sbuf", [128, 8], I32), "pl": ("sbuf", [128, 8], U16),
    "t0": ("psum", [128, 512], F32), "t1": ("psum", [128, 512], F32), "t2": ("psum", [128, 512], F32),
    "t3": ("psum", [128, 512], F32),
    "w0": ("psum", [128, 1024], BF), "w1": ("psum", [128, 1024], BF), "w2": ("psum", [128, 1024], BF),
    "w3": ("psum", [128, 1024], BF),
}
SEMAPHORES = ("dpm dst den dtx dol doe dlist dle dfx df1 dy dcnt arrL arrF arrM0 arrM1 arrY loc "
              "gones gident gsel gpi g16 vst vrt vw0 vw1 vpad pf0 penc sac senc vhal vp1 vp5 "
              "win ps0 ps1 ps2 ps3 eg0 eg1 eg2 eg3 eg4 eg5 eg6 eg7 tx0 tx1 vx0 vx1 vl0 vl1 mx0 mx1 ta tb tc td mn0 mn1 mn2 mn3 g16b g24 srep "
              "pw0 pw1 pw2 pw3 vys pt sln0 sln1 vyi0 vyi1 vyf vflg pc scf").split()

PCUT = [("v", 736), ("s", 1408), ("s", 1984), ("v", 2048)]
PV = ["g0", "g3", "c1", "c3"]
PCUT1 = [("v", 256), ("s", 512), ("v", 896), ("s", 1408), ("s", 1920), ("v", 2048)]
PV1 = ["g0", "flags", "g2", "c1", "g5", "c3", "en", "c5"]
EG = [("v", 0, 4), ("v", 4, 5), ("v", 5, 8), ("s", 8, 13), ("s", 13, 16)]
SETS = [(0, 4), (4, 8), (8, 13), (13, 16)]
BANKS = [("s", 0, 2), ("v", 2, 4), ("s", 4, 5), ("v", 5, 8)]
EV = ["g0", "g2", "g1", "m0", "m2", "m3", "m1", "w1", "w3"]
ES = ["g3", "g4", "w0", "w2"]
EP = ["g0", "g3", "g2", "g4", "g1", "w0", "w1", "w3", "w2"]
XBANKS = [("s", 0, 3), ("v", 3, 4), ("v", 4, 7), ("s", 7, 8)]
FG = [("v", 0, 2), ("s", 8, 11), ("v", 2, 4), ("s", 11, 12), ("v", 4, 6), ("s", 12, 15), ("v", 6, 8), ("s", 15, 16)]
FSHIP = 6
LG = [("v", 0, 4), ("s", 4, 9), ("v", 9, 12), ("s", 12, 15), ("v", 15, 16)]
LSETS = [(0, 12), (12, 16)]


def rank_program(g, core, T, topo):
    me = T.rank_of(core)
    if me is None:
        return
    ve, se, pe, sy = g.vector, g.scalar, g.tensor, g.sync
    Q = {"v": ve, "s": se, "p": pe, "y": sy, "g": g}
    n = {s: 0 for s in SEMAPHORES}
    seen = {}

    def inc(ins, name, k=1):
        ins.then_inc(T.sem[name], k)
        n[name] += k

    def wait(q, *names):
        for s in names:
            if seen.get((q, s), 0) < n[s]:
                Q[q].wait_ge(T.sem[s], n[s])
                seen[(q, s)] = n[s]

    def ring(src):
        far = [c for c in T.cores if topo.die(c) != topo.die(src)]
        near = [c for c in T.cores if topo.die(c) == topo.die(src) and c != src]
        turn = T.rank_of(src) % len(far)
        far = far[turn:] + far[:turn]
        out = []
        while far or near:
            if far:
                out.append(far.pop(0))
            if near:
                out.append(near.pop(0))
        return out
    others = [c for c in T.cores if c != core]
    order = ring(core)

    def first_of_die(c):
        return min(T.rank_of(d) for d in T.cores if topo.die(d) == topo.die(c))

    def did(c):
        rid, pid, _s = topo.addr(c)
        return DstId(rid=rid, pnc=pid)

    def to_all(ap, arr):
        m = topo.mask(core, order[0])
        for c in order:
            m &= topo.mask(core, c)
        g.remote_dma_fused([RemoteDMATransfer(dst_ids=[did(c) for c in order], dma_engine_mask=m, remote_sem=T.sem[arr],
                                              srcs=[ap], dsts=[ap for c in order])], local_sem=T.sem.loc)
        n["loc"] += bin(m).count("1")
        n[arr] += bin(m).count("1") * len(order)

    def each(tx, rx, arr):
        trs = []
        for k, c in enumerate(order):
            e = topo.engines(core, c)
            half = len(e) // 2
            m = sum((1 << e[i]) | (1 << e[i + half]) for i in ([k] if k else [k] + list(range(len(order), half))))
            trs.append(RemoteDMATransfer(dst_ids=[did(c)], dma_engine_mask=m, remote_sem=T.sem[arr],
                                         src=tx[T.rank_of(c)], dst=rx[me]))
            n["loc"] += bin(m).count("1")
        g.remote_dma_fused(trs, local_sem=T.sem.loc)
        n[arr] += sum(4 if ring(c)[0] == core else 2 for c in others)

    def by_die(arr, src_of, dst_of):
        trs = []
        for k, across in enumerate((True, False)):
            to = [c for c in order if (topo.die(c) != topo.die(core)) == across]
            e = topo.engines(core, to[0])[k::2]
            trs.append(RemoteDMATransfer(dst_ids=[did(c) for c in to], dma_engine_mask=sum(1 << i for i in e),
                                         remote_sem=T.sem[arr], srcs=[src_of(to[0])], dsts=[dst_of(c) for c in to]))
            n["loc"] += len(e)
            n[arr] += len(e) * len(to)
        g.remote_dma_fused(trs, local_sem=T.sem.loc)

    def gather(q, out, win, off, name):
        if q == "v":
            inc(ve.tensor_copy(out, win.indirect(off)), name)
        else:
            inc(se.activation(out, win.indirect(off), F.Copy), name)

    def places(cut, vector_order, plc, pmo, flags, ready, scalar_gap=None):
        for q in "vs":
            wait(q, *ready)
        lo = [0] + [e for _q, e in cut]
        ends = [int(op[1]) for op in vector_order if op[0] == "c"]

        def piece(k):
            a, b = lo[k], lo[k + 1]
            gather(cut[k][0], plc[:, a:b], T.win[:], pmo[:, a // 16:b // 16], "ps%d" % len([e for e in ends if e < k]))
        for k in range(len(cut)):
            if cut[k][0] == "s":
                piece(k)
        if scalar_gap:
            scalar_gap()
        done, scans = 0, 0
        for op in vector_order:
            if op in ("flags", "en"):
                flags_turned() if op == "flags" else en_offsets()
                continue
            k = int(op[1])
            if op[0] == "g":
                piece(k)
                continue
            a, b = lo[done], lo[k + 1]
            marks = flags(a, b)
            wait("v", "ps%d" % scans)
            inc(ve.tensor_tensor_scan(T.cls[:, a:b], marks, plc[:, a:b],
                                      T.cls[:, a - 1:a] if scans else 1.0, A.max, A.min), "ps%d" % (scans + 1))
            done, scans = k + 1, scans + 1
        for q in "vs":
            wait(q, "ps%d" % scans)
        return "ps%d" % scans

    own = slice(16 * me, 16 * me + 16)
    inc(sy.dma_start(T.pmi[:], T.pm[:]), "dpm", 16)
    inc(sy.dma_start(T.sti[:], T.st[:]), "dst", 16)
    inc(sy.dma_start(T.ptx[:, 0:64, :], T.pm[:]), "dtx", 16)
    inc(sy.dma_start(T.ptx[:, 64:128, :], T.en[:]), "dtx", 16)
    inc(sy.dma_start(T.eni[:], T.en[:]), "den", 16)
    inc(ve.memset(T.ratio[:], RHO), "vrt")

    def ones(k):
        return T.stt[:, 128:128 + k]
    inc(g.iota(ones(192), [[0, 192]], 1, 0, allow_small_or_imprecise_dtypes=True), "gones")
    wait("g", "gones")
    inc(g.affine_select(T.ident[:], ones(128), [[-1, 128]], A.is_equal, 0.0, 0, 1), "gident")
    inc(g.affine_select(T.sel[:], ones(32), [[0, 2], [-8, 16]], A.is_equal, 0.0, 0, 1), "gsel")
    sel8 = T.sel[:, 0:16:2]
    wait("v", "vrt")
    inc(ve.tensor_tensor_scan(T.win[:, 0:256], T.ratio[:], T.ratio[:], RHO ** (-V - 1), A.mult, A.min), "vw0")
    wait("v", "vw0")
    wait("s", "vw0")
    for k in range(1, 8):
        dst, f = T.win[:, 256 * k:256 * k + 256], RHO ** (256 * k)
        if k < SWIN:
            inc(ve.tensor_scalar(dst, T.win[:, 0:256], f, None, A.mult), "win")
        else:
            inc(se.activation(dst, T.win[:, 0:256], F.Copy, scale=f), "win")
    wait("v", "dpm")
    inc(ve.tensor_copy(T.pmo[:], T.pmi[:]), "win")
    wait("v", "dst")
    inc(ve.tensor_copy(T.stb[:], T.sti[:]), "vst")
    wait("p", "vst", "gident")
    inc(pe.transpose(T.w2[:, 0:128], T.stb[:], T.ident[:]), "pf0")
    fend = [PCUT1[int(op[1])][1] for op in PV1 if op[0] == "c"]

    def flag_bank(a):
        s = len([e for e in fend if e <= a])
        return s, T["w%d" % (0, 1, 3)[s]], ([0] + fend)[s]

    def flags_turned():
        wait("v", "pf0")
        inc(ve.tensor_copy(T.stt[:, 0:128], T.w2[:, 0:128]), "vpad")
        wait("p", "vpad")
        for k in range(16):
            s, bank, lo = flag_bank(128 * k)
            inc(pe.transpose(bank[:, 128 * k - lo:128 * k - lo + 128], T.stt[:, k:k + 128], T.ident[:]), "ps%d" % s)
        for b in range(16):
            inc(pe.matmul(T.t2[:, b:128:16], T.win[:, 128 * b:128 * b + 128], sel8, True, True), "penc")
    wait("g", "dtx")
    each(T.ptx, T.prx, "arrL")
    inc(g.iota(T.pi[:], [[1, 8]], 8 * (me - first_of_die(core)), 32), "gpi")
    inc(g.affine_select(T.m16[:, 0:64], ones(64), [[0, 4], [1, 16]], A.is_equal, 0.0, 0, 0), "g16")
    mine = slice(32 * (me - first_of_die(core)), 32 * (me - first_of_die(core)) + 32)
    wait("y", "dtx")
    inc(sy.dma_start(T.prx[me], T.ptx[me]), "dol", 16)
    wait("p", "gsel", "win")

    def idle_columns(*pairs):
        wait("s", "gones")
        for b in pairs:
            inc(se.activation(T.plc[:, 384 * b + 256:384 * b + 384], ones(128), F.Copy), "srep")

    def en_offsets():
        wait("v", "den")
        inc(ve.tensor_copy(T.eno[:], T.eni[:]), "ps3")

    def bank_flags(a, b):
        return flag_bank(a)[1][:, 0:b - a]

    scanned = places(PCUT1, PV1, T.stm, T.pmo, bank_flags, ("win",), lambda: idle_columns(5, 6))
    wait("y", "vst")
    inc(sy.dma_start(T.ftx[:], T.stb[:]), "dfx", 16)
    inc(sy.dma_start(T.frx[me, mine, :], T.stb[own, :]), "doe", 16)
    wait("y", "dol", "arrL")
    inc(sy.dma_start(T.pmi2[:], T.prx[:, 0:64, :]), "dlist", 16)
    inc(sy.dma_start(T.eni2[:], T.prx[:, 64:128, :]), "dle", 16)

    def vertices(piece, name, eno):
        q, b0, b1 = piece
        gather(q, T.ver[:, 128 * b0:128 * b1], T.cls[:], eno[:, 8 * b0:8 * b1], name)

    def slab(s, *pieces):
        for name, b0, b1 in pieces:
            wait("p", name, "gsel")
            for b in range(b0, b1):
                j = b % 4 + 4 * (b // 8)
                inc(pe.matmul(T["t%d" % s][:, j:64:8], T.ver[:, 128 * b:128 * b + 128], sel8, True, True), "tx%d" % s)

    def ship(s):
        x = T["x%d" % s]
        wait("v", "tx%d" % s)
        base = 0 if first_of_die(core) else 256
        inc(ve.tensor_copy(x[:, base:base + 64], T["t%d" % s][:, 0:64]), "vx%d" % s)
        wait("g", "vx%d" % s)

        def cols(a):
            return x[:, a:a + 32]
        by_die("arrM%d" % s, lambda c: cols(base + 8 * first_of_die(c)),
               lambda c: cols((32 if first_of_die(c) else 0) + 32 * ((me - T.rank_of(c)) % 8)))

    for k, p in enumerate(FG):
        if k == FSHIP:
            ship(0)
        vertices(p, "eg%d" % k, T.eno)
        slab(p[1] % 8 // 4, ("eg%d" % k, p[1], p[2]))
    ship(1)
    wait("g", "dfx")
    by_die("arrF", lambda c: T.ftx[min(first_of_die(c), 1)], lambda c: T.frx[me])
    wait("y", "arrF", scanned, "doe")
    for h in (0, 8):
        inc(sy.dma_start(T.stm[h:128:16, :], T.frx[:, mine, :]), "df1", 16)
    inc(g.affine_select(T.m24[:], ones(192), [[0, 8], [1, 24]], A.is_equal, 0.0, 0, 0), "g24")
    inc(g.affine_select(T.m16[:, 64:192], ones(128), [[0, 8], [1, 16]], A.is_equal, 0.0, 0, 0), "g16b")
    wait("v", "gpi", "penc")
    inc(ve.tensor_scalar(T.pa[:], T.pi[:], 255, None, A.bitwise_and), "vp1")
    for h in (0, 1):
        inc(ve.tensor_reduce(T.hal[:, h:h + 1], T.sel[:, h:16:2], AxisListType.X, A.max), "vhal")
    wait("v", "vp1")
    inc(ve.tensor_copy(T.pl[:], T.pa[:]), "vp5")
    wait("v", "dlist")
    inc(ve.tensor_copy(T.pmo2[:], T.pmi2[:]), "win")
    wait("v", "g16", "vp5", "vhal")
    wait("p", "gident")
    inc(se.activation(T.lnc[:, 0:2], ones(2), F.Ln, scale=math.exp(0.5 / math.log(RHO)),
                      accum_out=T.acol[:, 0:1]), "sac")
    wait("s", "vhal")

    def spread(banks, k, rep, first, step, *ready):
        _q, b0, b1 = banks[k]
        wait("p", *ready)
        for b in range(b0, b1):
            c = first + step * b
            inc(pe.transpose(T["w%d" % k][:, 128 * (b - b0):128 * (b - b0 + 1)], rep[:, c:c + 128], T.ident[:]),
                "pw%d" % k)

    def window(banks, k):
        q, b0, b1 = banks[k]
        src = T["w%d" % k][:, 0:128 * (b1 - b0)]
        wait(q, "pw%d" % k)
        for h in (0, 1):
            dst, blank = T.win[:, 1024 * h + 128 * b0:1024 * h + 128 * b1], T.hal[:, 1 - h:2 - h]
            if q == "v":
                inc(ve.tensor_scalar(dst, src, blank, None, A.max), "win")
            else:
                inc(se.activation(dst, src, F.Identity, bias=blank), "win")

    for s in (0, 1):
        lr = T["lr%d" % s]
        wait("v", "vx0", "vx1", "arrM%d" % s)
        for h in (0, 1):
            gather("v", lr[:, 64 * h:64 * h + 64], T["x%d" % s][:, 32:288], T.pl[:, 4 * h:4 * h + 4], "vl%d" % h)
        for h in (0, 1):
            c = 1024 * s + 8 * h
            wait("v", "vl%d" % h)
            inc(ve.tensor_tensor_scan(T.cls[:, c:c + 1016:16], T.m16[:, 0:64], lr[:, 64 * h:64 * h + 64],
                                      1.0, A.max, A.min), "mx%d" % s)
        for k in (2 * s, 2 * s + 1):
            spread(XBANKS, k, T.cls, 128, 256, "mx%d" % s)
        if not s:
            wait("v", "dle")
            inc(ve.tensor_copy(T.eno2[:], T.eni2[:]), "win")
    for k in range(len(XBANKS)):
        window(XBANKS, k)

    def set_of(sets, b):
        return [s for s, (b0, b1) in enumerate(sets) if b0 <= b < b1][0]

    def turn(pieces, k, sets, wide, names):
        _q, b0, b1 = pieces[k]
        s = set_of(sets, b0)
        wait("p", "senc", "eg%d" % k)
        for b in range(b0, b1):
            c = wide * (b - sets[s][0])
            inc(pe.matmul(T["t%d" % s][:, c:c + wide], T.ver[:, 128 * b:128 * b + 128], T.sel[:, 0:wide], True, True),
                names[s])

    def row_flags(a, b):
        wait("v", "df1")
        return T.stm[:, a:b]

    def codes_and_columns():
        wait("s", "penc")
        inc(se.activation(T.enc[:], T.t2[:, 0:128], F.Copy), "senc")
        idle_columns(7)

    for hop in (2, 3):
        places(PCUT, PV, T.plc, T.pmo2, row_flags, ("win",), codes_and_columns if hop == 2 else None)
        todo = {"v": list(EV), "s": list(ES), "p": list(EP)}
        made = set()
        while todo["v"] or todo["s"] or todo["p"]:
            for q in "vsp":
                while todo[q]:
                    op = todo[q][0]
                    k = int(op[1])
                    if q == "p" and op[0] == "w":
                        need = sorted(set("m%d" % set_of(SETS, b + h) for b in range(*BANKS[k][1:]) for h in (0, 8)))
                    elif q == "p":
                        need = [op]
                    elif op[0] == "m":
                        need = ["pg%d" % j for j in range(len(EG)) if set_of(SETS, EG[j][1]) == k]
                    else:
                        need = ["p" + op] if op[0] == "w" else []
                    if not all(x in made for x in need):
                        break
                    todo[q].pop(0)
                    made.add("p" + op if q == "p" else op)
                    if q == "p" and op[0] == "w":
                        spread(BANKS, k, T.plc, 256, 384, "srep", *["mn" + x[1] for x in need])
                    elif q == "p":
                        turn(EG, k, SETS, 24, ("ta", "tb", "tc", "td"))
                    elif op[0] == "g":
                        vertices(EG[k], "eg%d" % k, T.eno2)
                    elif op[0] == "w":
                        window(BANKS, k)
                    else:
                        b0, b1 = SETS[k]
                        wait("v", "g24", "srep", ("ta", "tb", "tc", "td")[k])
                        c = 384 * (b0 % 8) + 8 * (b0 // 8)
                        inc(ve.tensor_tensor_scan(T.plc[:, c:c + 384 * (b1 - b0) - 8:16],
                                                  T.m24[:, 0:24 * (b1 - b0)], T["t%d" % k][:, 0:24 * (b1 - b0)],
                                                  1.0, A.max, A.min), "mn%d" % k)

    places(PCUT, PV, T.plc, T.pmo2, row_flags, ("win",))
    for k in range(len(LG)):
        vertices(LG[k], "eg%d" % k, T.eno2)
        turn(LG, k, LSETS, 16, ("ta", "tb"))
    for s, (b0, b1) in enumerate(LSETS):
        c = 16 * (b1 - b0)
        wait("v", "g16b", ("ta", "tb")[s])
        inc(ve.tensor_tensor_scan(T.red[:, 16 * b0:16 * b1], T.m16[:, 0:c], T["t%d" % s][:, 0:c], 1.0, A.max, A.min),
            "mn0")
    wait("v", "mn0")
    inc(ve.tensor_copy(T.land2[:, own], T.red[:, 15:256:16]), "vys")

    wait("g", "vys")
    to_all(T.land2[:, own], "arrY")
    wait("p", "vys", "arrY")
    inc(pe.transpose(T.w0[:, 0:128], T.land2[:], T.ident[:]), "pt")
    wait("v", "senc", "sac", "vys", "arrY")
    inc(ve.tensor_tensor(T.flg[:], T.land2[:], T.enc[:], A.is_equal), "vflg")
    wait("s", "pt")
    halves = [(h, slice(64 * h, 64 * h + 64)) for h in (0, 1)]
    for h, c in halves:
        inc(se.activation(T.lnv[:, c], T.w0[:, c], F.Ln, scale=RHO ** 1024), "sln%d" % h)
    for h, c in halves:
        wait("v", "sln%d" % h, "sac")
        inc(ve.tensor_scalar(T.yi[:, c], T.lnv[:, c], T.acol[:, 0:1], 1024.0, A.mult, A.add), "vyi%d" % h)
    for h, c in halves:
        wait("v", "vyi%d" % h)
        inc(ve.tensor_copy(T.yf[:, c], T.yi[:, c]), "vyf")
    wait("y", "vyf")
    inc(sy.dma_start(T.y[:], T.yf[:]), "dy", 16)
    wait("p", "vflg")
    for b in range(16):
        pc = pe.matmul(T.t3[0:8, 0:1], T.flg[:, b:128:16], ones(1), b == 0, b == 15)
    inc(pc, "pc")
    wait("s", "pc")
    inc(se.activation(T.cf[0:8, 0:1], T.t3[0:8, 0:1], F.Copy), "scf")
    wait("s", "scf")
    inc(se.dma_start(T.cnt[:], T.cf[0:8, 0:1]), "dcnt", 16)
    wait("y", "dy")
    wait("s", "dcnt")
    wait("g", "loc")
